import numpy as np
import ml_dtypes


def mxq(x, axis, fmt="e4m3"):
    dtype, down = {"e4m3": (ml_dtypes.float8_e4m3fn, 7), "e5m2": (ml_dtypes.float8_e5m2, 14)}[fmt]
    v = np.moveaxis(np.asarray(x, np.float32).astype(ml_dtypes.bfloat16).astype(np.float64), axis, -1)
    blocks = v.reshape(v.shape[:-1] + (-1, 32))
    amax = np.abs(blocks).max(-1, keepdims=True)
    byte = np.maximum(np.where(amax > 0, np.frexp(amax)[1] - 1 + 127, 0) - down, 1)
    scale = np.exp2(byte - 127.0)
    codes = (blocks / scale).astype(np.float32).astype(dtype).astype(np.float64)
    return np.moveaxis((codes * scale).reshape(v.shape), -1, axis)


WIDE = False


def mx_kscale(k):
    if not WIDE:
        return np.ones(k)
    levels = np.array([10, -10, 5, -5, 0])
    if k % 512:
        return np.exp2(np.random.permutation(np.resize(levels, k // 32))).repeat(32)
    a = np.empty((k // 512, 16))
    for p in range(k // 512):
        a[p, :8] = np.random.permutation(np.resize(levels, 8))
        for g in range(8):
            far = levels[np.abs(levels - a[p, g]) >= 10]
            a[p, g + 8] = far[np.random.randint(len(far))]
    return np.exp2(a.ravel()).repeat(32)


def f64(x):
    return np.asarray(x).astype(np.float64)


def striped(idx):
    return np.tile(idx.reshape(-1, 16).T, (8, 1)).astype(np.uint16)


def unstriped(offs):
    return offs[:16].T.reshape(-1).astype(np.int64)


E2M1 = np.array([0.0, 0.5, 1.0, 1.5, 2.0, 3.0, 4.0, 6.0, -0.0, -0.5, -1.0, -1.5, -2.0, -3.0, -4.0, -6.0])


def pack_weight(w, fmt):
    k, n = w.shape
    w = f64(np.asarray(w, np.float32).astype(ml_dtypes.bfloat16)).reshape(k // 32, 32, n)
    amax = np.abs(w).max(1)
    if fmt == "e4m3":
        byte = np.frexp(amax)[1] - 1 + 127 - 7
    else:
        mant, ex = np.frexp(amax / 6.0)
        byte = np.where(mant > 0.5, ex, ex - 1) + 127
    byte = np.clip(np.where(amax > 0, byte, 1), 1, 254)
    scaled = (w * np.exp2(127.0 - byte)[:, None, :]).reshape(k, n).astype(np.float32)
    by_word = np.ascontiguousarray(scaled.reshape(k // 512, 128, 4, n).transpose(0, 1, 3, 2))
    if fmt == "e4m3":
        words = by_word.astype(ml_dtypes.float8_e4m3fn).view(np.uint8)
    else:
        c = by_word.astype(ml_dtypes.float4_e2m1fn).view(np.uint8) & 0xF
        words = (c[..., 0::2] | (c[..., 1::2] << 4)).reshape(k // 512, 128, 2 * n)
    return np.ascontiguousarray(words), np.ascontiguousarray(byte.astype(np.uint8).reshape(k // 512, 16, n))


def unpack_weight(words, scales, fmt):
    g, _, n = scales.shape
    words = np.ascontiguousarray(words).reshape(g, 128, n, -1)
    if fmt == "e4m3":
        vals = words.view(ml_dtypes.float8_e4m3fn).astype(np.float64)
    else:
        nib = np.empty((g, 128, n, 4), np.uint8)
        nib[..., 0::2] = words & 0xF
        nib[..., 1::2] = words >> 4
        vals = E2M1[nib]
    vals = vals * np.repeat(np.exp2(scales.astype(np.float64) - 127.0), 8, axis=1)[..., None]
    return vals.transpose(0, 1, 3, 2).reshape(g * 512, n)


K, T, E, C, N = 2048, 640, 15, 128, 128
TOP = 3
K8 = 1024


def by_expert(wq, xq):
    return np.concatenate([wq[e].T @ xq[:, e * C:(e + 1) * C] for e in range(E)], axis=1)


def setup_inputs():
    n = np.random.standard_normal
    s = mx_kscale(K)[:, None]
    deal = np.repeat(np.arange(E), C).reshape(TOP, T)[:, np.random.permutation(T)]
    deal = np.take_along_axis(deal, np.argsort(np.random.rand(TOP, T), axis=0), axis=0)
    for _ in range(8):
        s_, t_ = np.random.permutation(T).reshape(2, -1); r = np.random.randint(TOP, size=T // 2); x, y = deal[r, s_].copy(), deal[r, t_].copy()
        ok = ~((deal[:, s_] == y).any(0) | (deal[:, t_] == x).any(0)); deal[r[ok], s_[ok]] = y[ok]; deal[r[ok], t_[ok]] = x[ok]
    order = np.lexsort((np.random.rand(TOP * T), deal.reshape(-1)))
    slot_token = order % T; pos = np.empty(TOP * T, np.int64); pos[order] = np.arange(TOP * T); pos = pos.reshape(TOP, T)
    g = np.random.uniform(0.5, 1.5, (TOP, T)); g = g / g.sum(0)
    w = n((E, K, N)) / np.sqrt(K) / s[None]
    w8 = [pack_weight(m[:K8], "e4m3") for m in w]
    w4 = [pack_weight(m[K8:], "e2m1") for m in w]
    return {
        "xT": (n((K, T)) * s).astype(np.float32),
        "w8_words": np.stack([m[0] for m in w8]),
        "w8_scales": np.stack([m[1] for m in w8]),
        "w4_words": np.stack([m[0] for m in w4]),
        "w4_scales": np.stack([m[1] for m in w4]),
        "gate": np.stack([np.tile(r, (N, 1)) for r in g]).astype(np.float32),
        "offs": striped(slot_token),
        "pos1": striped(pos[0]),
        "pos2": striped(pos[1]),
        "pos3": striped(pos[2]),
    }


def reference(xT, w8_words, w8_scales, w4_words, w4_scales, gate, offs, pos1, pos2, pos3):
    idx = unstriped(offs)
    w = np.stack([np.concatenate([unpack_weight(w8_words[e], w8_scales[e], "e4m3"), unpack_weight(w4_words[e], w4_scales[e], "e2m1")]) for e in range(E)])
    xq = mxq(f64(xT)[:, idx], 0, "e4m3")
    y = by_expert(w, xq)
    return sum(f64(gate[r]) * y[:, unstriped(p)] for r, p in enumerate((pos1, pos2, pos3)))

@@ -1,0 +1,194 @@
+from contextlib import ExitStack
+
+import concourse.mybir as mybir
+
+K, T, E, C, N = 2048, 640, 15, 128, 128
+TOP = 3
+S = E * C
+FLOPS = 2 * K * N * S
+
+F32 = mybir.dt.float32
+BF16 = mybir.dt.bfloat16
+I32 = mybir.dt.int32
+U32 = mybir.dt.uint32
+U16 = mybir.dt.uint16
+U8 = mybir.dt.uint8
+FP8X4 = mybir.dt.float8_e4m3fn_x4
+FP4X4 = mybir.dt.float4_e2m1fn_x4
+MULT = mybir.AluOpType.mult
+ADD = mybir.AluOpType.add
+
+P = 128
+PACK = 4
+K_PASS = P * PACK
+PASSES = K // K_PASS
+HALF = PASSES // 2
+LIST_ROWS = 16
+PLANE_ROW = (4, 12, 0, 8)
+W8_ROW = 4
+HELD_WINDOW = 1024
+EARLY_CUT = (0, 480, 960, 1440, 1920)
+EXPERT_CUT = (0, 3, 6, 9, 12, 14, 15)
+WEIGHT_CUT = (0, 5, 10, 15)
+LOAD_CUT = ((0, 256, 512, 640), (0, 256, 640), (0, 640), (0, 384, 640))
+QUANT_CUT = ((0, 256, 512, 640), (0, 512, 640), (0, 512, 640), (0, 512, 640))
+TOKEN_CUT = (0, 320, 640)
+
+
+def spans(cut):
+    return list(zip(cut[:-1], cut[1:]))
+
+
+def tile_moe_tk_lin_none_kernel(
+    tc, xT, w8_words, w8_scales, w4_words, w4_scales, gate, offs, pos1, pos2, pos3, out
+):
+    nc = tc.nc
+    with ExitStack() as ctx:
+        lists = ctx.enter_context(tc.tile_pool(name="lists", bufs=1))
+        keep = ctx.enter_context(tc.tile_pool(name="keep", bufs=1))
+        psum = ctx.enter_context(tc.psum_pool(name="psum", bufs=1))
+
+        slot_token = lists.tile([P, S // LIST_ROWS], U16, name="slot_token")
+        token_slot = [lists.tile([P, T // LIST_ROWS], U16, name="token_slot%d" % r) for r in range(TOP)]
+
+        x_raw = [
+            [
+                keep.tile([P, PACK, t1 - t0], F32, name="x_raw%d_%d" % (a, t0), tag="stage%d_%d" % (a, t0), align_bytes=64)
+                for t0, t1 in spans(LOAD_CUT[a])
+            ]
+            for a in range(PASSES)
+        ]
+        x_bf = [keep.tile([P, T, PACK], BF16, name="x_bf%d" % a, align_bytes=64) for a in range(PASSES)]
+        early_words = [keep.tile([P, T], U32, name="early_words%d" % a, align_bytes=64) for a in range(HALF)]
+        late_words = keep.tile([P, HALF * T], U32, name="late_words", align_bytes=64)
+        tok_words = [early_words[0][:], early_words[1][:], late_words[:, 0:T], late_words[:, T : 2 * T]]
+        windows = [early_words[0][:], early_words[1][:], late_words[:, 0:HELD_WINDOW], late_words[:, T : 2 * T]]
+        tok_scales = keep.tile([P, T], U8, name="tok_scales", align_bytes=64)
+        slot_words = [keep.tile([P, S], U32, name="slot_words%d" % a, align_bytes=64) for a in range(PASSES)]
+        slot_scales = keep.tile([P, S], U8, name="slot_scales", align_bytes=64)
+        last_scales = keep.tile([P, S], U8, name="last_scales", align_bytes=64)
+        y = keep.tile([P, S], F32, name="y")
+        terms = [keep.tile([P, T], F32, name="term%d" % r) for r in range(TOP)]
+        partial = keep.tile([P, T], F32, name="partial")
+        result = keep.tile([P, T], F32, name="result")
+
+        for plane in (tok_scales, last_scales):
+            nc.vector.memset(plane[:].bitcast(I32), 0)
+
+        for a in range(PASSES):
+            rows = xT[a * K_PASS : (a + 1) * K_PASS, :].rearrange("(p j) t -> p j t", j=PACK)
+            for raw, (t0, t1) in zip(x_raw[a], spans(LOAD_CUT[a])):
+                nc.sync.dma_start(raw[:], rows[:, :, t0:t1])
+            if a == 0:
+                nc.sync.dma_start(slot_token[:], offs)
+        for tile, pos in zip(token_slot, (pos1, pos2, pos3)):
+            nc.sync.dma_start(tile[:], pos)
+
+        def round_tokens(a, piece):
+            t0, t1 = spans(LOAD_CUT[a])[piece]
+            dst = x_bf[a][:, t0:t1, :].rearrange("p (c i) j -> p c j i", i=4)
+            src = x_raw[a][piece][:].rearrange("p j (c i) -> p c j i", i=4)
+            if a == 0:
+                nc.vector.tensor_copy(dst, src)
+            else:
+                nc.scalar.copy(dst, src)
+
+        def quantize_tokens(a, piece):
+            t0, t1 = spans(QUANT_CUT[a])[piece]
+            nc.vector.quantize_mx(
+                out=tok_words[a][:, t0:t1].bitcast(FP8X4),
+                scales=tok_scales[PLANE_ROW[a] : P, t0:t1],
+                in_=x_bf[a][:, t0:t1, :].rearrange("p t j -> p (t j)"),
+            )
+
+        def gather(dst, window, s0, s1):
+            offsets = slot_token[:, s0 // LIST_ROWS : s1 // LIST_ROWS]
+            nc.vector.tensor_copy(dst[:, s0:s1], window.indirect(offsets))
+
+        round_tokens(0, 0)
+        quantize_tokens(0, 0)
+        round_tokens(0, 1)
+        round_tokens(0, 2)
+        quantize_tokens(0, 1)
+        quantize_tokens(0, 2)
+        for a in range(1, PASSES):
+            for piece in range(len(x_raw[a])):
+                round_tokens(a, piece)
+
+        stage_tags = ["stage%d_%d" % (a, t0) for a in range(PASSES) for t0, t1 in spans(LOAD_CUT[a])]
+        w_scales = keep.tile([P, E * HALF * N], U8, name="w_scales", tag=stage_tags.pop(2), align_bytes=64)
+        nc.gpsimd.memset(w_scales[:].bitcast(I32), 0)
+        dst = w_scales[:].bitcast(I32).rearrange("p (m n) -> p m n", n=N // 4)
+        for row, scales in ((W8_ROW, w8_scales), (0, w4_scales)):
+            src = scales.bitcast(I32).rearrange("e a (q r) n -> r q (e a) n", r=4)
+            for r in range(4):
+                nc.gpsimd.dma_start(dst[row + r : P : 32], src[r])
+
+        w8_src = w8_words.rearrange("e a p n t -> p (e a) (n t)").bitcast(I32)
+        w4_src = w4_words.rearrange("e a p b -> p (e a) b").bitcast(I32)
+        w8, w4 = {}, {}
+        for g, (e0, e1) in enumerate(spans(WEIGHT_CUT)):
+            rows = slice(HALF * e0, HALF * e1)
+            w8_tile = keep.tile([P, HALF * (e1 - e0), N * 4], U8, name="w8_%d" % g, tag=stage_tags[2 * g], align_bytes=64)
+            w4_tile = keep.tile([P, HALF * (e1 - e0), N * 2], U8, name="w4_%d" % g, tag=stage_tags[2 * g + 1], align_bytes=64)
+            nc.sync.dma_start(w8_tile[:].bitcast(I32), w8_src[:, rows, :])
+            nc.sync.dma_start(w4_tile[:].bitcast(I32), w4_src[:, rows, :])
+            for m in range(HALF * e0, HALF * e1):
+                w8[m] = w8_tile[:, m - HALF * e0, :].bitcast(FP8X4)
+                w4[m] = w4_tile[:, m - HALF * e0, :].bitcast(FP4X4)
+        gates = keep.tile([P, TOP, T], F32, name="gates", tag=stage_tags[-1], align_bytes=64)
+        nc.sync.dma_start(gates[:], gate.rearrange("r n t -> n r t"))
+
+        for a in range(HALF):
+            for s0, s1 in spans(EARLY_CUT):
+                if s1 == S:
+                    for piece in range(2):
+                        quantize_tokens(a + 1, piece)
+                gather(slot_words[a], windows[a], s0, s1)
+        for piece in range(2):
+            quantize_tokens(PASSES - 1, piece)
+
+        def gather_scales(half):
+            cut = EARLY_CUT[2 * half : 2 * half + 3]
+            for s0, s1 in spans(cut):
+                gather(slot_scales, tok_scales[:], s0, s1)
+            cols = slice(cut[0] // 4, cut[-1] // 4)
+            row = PLANE_ROW[PASSES - 1]
+            nc.scalar.dma_start(last_scales[:].bitcast(I32)[0 : P - row, cols], slot_scales[:].bitcast(I32)[row:P, cols])
+
+        for e0, e1 in spans(EXPERT_CUT):
+            if e0 < EXPERT_CUT[2]:
+                gather_scales(EXPERT_CUT.index(e0))
+            for a in range(HALF, PASSES):
+                gather(slot_words[a], windows[a], e0 * C, e1 * C)
+            bank = psum.tile([P, (e1 - e0) * C], F32, name="bank%d" % e0)
+            for e in range(e0, e1):
+                slots = slice(e * C, (e + 1) * C)
+                for a in range(PASSES):
+                    m = HALF * e + a % HALF
+                    if a < HALF:
+                        weights, w_row = w8[m], W8_ROW
+                    else:
+                        weights, w_row = w4[m], 0
+                    if a == PASSES - 1:
+                        x_plane = last_scales[:, slots]
+                    else:
+                        x_plane = slot_scales[PLANE_ROW[a] : P, slots]
+                    nc.tensor.matmul_mx(
+                        out=bank[:, (e - e0) * C : (e - e0 + 1) * C],
+                        lhsT=weights,
+                        lhsT_scale=w_scales[w_row:P, m * N : (m + 1) * N],
+                        rhs=slot_words[a][:, slots].bitcast(FP8X4),
+                        rhs_scale=x_plane,
+                        start=(a == 0),
+                        stop=(a == PASSES - 1),
+                    )
+            nc.scalar.copy(y[:, e0 * C : e1 * C], bank[:])
+
+        for t0, t1 in spans(TOKEN_CUT):
+            for r in range(TOP):
+                offsets = token_slot[r][:, t0 // LIST_ROWS : t1 // LIST_ROWS]
+                nc.vector.tensor_tensor(terms[r][:, t0:t1], y[:].indirect(offsets), gates[:, r, t0:t1], MULT)
+            nc.vector.tensor_tensor(partial[:, t0:t1], terms[0][:, t0:t1], terms[1][:, t0:t1], ADD)
+            nc.vector.tensor_tensor(result[:, t0:t1], partial[:, t0:t1], terms[2][:, t0:t1], ADD)
+            nc.sync.dma_start(out[:, t0:t1], result[:, t0:t1])

@@ -67,12 +67,13 @@ def tile_moe_tk_lin_none_kernel(
         slot_words = [keep.tile([P, S], U32, name="slot_words%d" % a, align_bytes=64) for a in range(PASSES)]
         slot_scales = keep.tile([P, S], U8, name="slot_scales", align_bytes=64)
         last_scales = keep.tile([P, S], U8, name="last_scales", align_bytes=64)
+        w_scales = keep.tile([P, E * HALF * N], U8, name="w_scales", align_bytes=64)
         y = keep.tile([P, S], F32, name="y")
         terms = [keep.tile([P, T], F32, name="term%d" % r) for r in range(TOP)]
         partial = keep.tile([P, T], F32, name="partial")
         result = keep.tile([P, T], F32, name="result")
 
-        for plane in (tok_scales, last_scales):
+        for plane in (w_scales, tok_scales, last_scales):
             nc.vector.memset(plane[:].bitcast(I32), 0)
 
         for a in range(PASSES):
@@ -83,6 +84,11 @@ def tile_moe_tk_lin_none_kernel(
                 nc.sync.dma_start(slot_token[:], offs)
         for tile, pos in zip(token_slot, (pos1, pos2, pos3)):
             nc.sync.dma_start(tile[:], pos)
+        dst = w_scales[:].bitcast(I32).rearrange("p (m n) -> p m n", n=N // 4)
+        for row, scales in ((W8_ROW, w8_scales), (0, w4_scales)):
+            src = scales.bitcast(I32).rearrange("e a (q r) n -> r q (e a) n", r=4)
+            for r in range(4):
+                nc.sync.dma_start(dst[row + r : P : 32], src[r])
 
         def round_tokens(a, piece):
             t0, t1 = spans(LOAD_CUT[a])[piece]
@@ -116,18 +122,12 @@ def tile_moe_tk_lin_none_kernel(
                 round_tokens(a, piece)
 
         stage_tags = ["stage%d_%d" % (a, t0) for a in range(PASSES) for t0, t1 in spans(LOAD_CUT[a])]
-        w_scales = keep.tile([P, E * HALF * N], U8, name="w_scales", tag=stage_tags.pop(2), align_bytes=64)
-        nc.gpsimd.memset(w_scales[:].bitcast(I32), 0)
-        dst = w_scales[:].bitcast(I32).rearrange("p (m n) -> p m n", n=N // 4)
-        for row, scales in ((W8_ROW, w8_scales), (0, w4_scales)):
-            src = scales.bitcast(I32).rearrange("e a (q r) n -> r q (e a) n", r=4)
-            for r in range(4):
-                nc.gpsimd.dma_start(dst[row + r : P : 32], src[r])
-
         w8_src = w8_words.rearrange("e a p n t -> p (e a) (n t)").bitcast(I32)
         w4_src = w4_words.rearrange("e a p b -> p (e a) b").bitcast(I32)
         w8, w4 = {}, {}
-        for g, (e0, e1) in enumerate(spans(WEIGHT_CUT)):
+
+        def load_weights(g):
+            e0, e1 = spans(WEIGHT_CUT)[g]
             rows = slice(HALF * e0, HALF * e1)
             w8_tile = keep.tile([P, HALF * (e1 - e0), N * 4], U8, name="w8_%d" % g, tag=stage_tags[2 * g], align_bytes=64)
             w4_tile = keep.tile([P, HALF * (e1 - e0), N * 2], U8, name="w4_%d" % g, tag=stage_tags[2 * g + 1], align_bytes=64)
@@ -136,8 +136,9 @@ def tile_moe_tk_lin_none_kernel(
             for m in range(HALF * e0, HALF * e1):
                 w8[m] = w8_tile[:, m - HALF * e0, :].bitcast(FP8X4)
                 w4[m] = w4_tile[:, m - HALF * e0, :].bitcast(FP4X4)
-        gates = keep.tile([P, TOP, T], F32, name="gates", tag=stage_tags[-1], align_bytes=64)
-        nc.sync.dma_start(gates[:], gate.rearrange("r n t -> n r t"))
+
+        load_weights(0)
+        load_weights(1)
 
         for a in range(HALF):
             for s0, s1 in spans(EARLY_CUT):
@@ -154,11 +155,14 @@ def tile_moe_tk_lin_none_kernel(
                 gather(slot_scales, tok_scales[:], s0, s1)
             cols = slice(cut[0] // 4, cut[-1] // 4)
             row = PLANE_ROW[PASSES - 1]
-            nc.scalar.dma_start(last_scales[:].bitcast(I32)[0 : P - row, cols], slot_scales[:].bitcast(I32)[row:P, cols])
+            nc.sync.dma_start(last_scales[:].bitcast(I32)[0 : P - row, cols], slot_scales[:].bitcast(I32)[row:P, cols])
 
+        for half in range(2):
+            gather_scales(half)
+        load_weights(2)
+        gates = keep.tile([P, TOP, T], F32, name="gates", tag=stage_tags[-2], align_bytes=64)
+        nc.sync.dma_start(gates[:], gate.rearrange("r n t -> n r t"))
         for e0, e1 in spans(EXPERT_CUT):
-            if e0 < EXPERT_CUT[2]:
-                gather_scales(EXPERT_CUT.index(e0))
             for a in range(HALF, PASSES):
                 gather(slot_words[a], windows[a], e0 * C, e1 * C)
             bank = psum.tile([P, (e1 - e0) * C], F32, name="bank%d" % e0)

@@ -26,11 +26,12 @@ HALF = PASSES // 2
 LIST_ROWS = 16
 PLANE_ROW = (4, 12, 0, 8)
 W8_ROW = 4
-HELD_WINDOW = 1024
-EARLY_CUT = (0, 480, 960, 1440, 1920)
-EXPERT_CUT = (0, 3, 6, 9, 12, 14, 15)
-WEIGHT_CUT = (0, 5, 10, 15)
-LOAD_CUT = ((0, 256, 512, 640), (0, 256, 640), (0, 640), (0, 384, 640))
+WORD_PLACE = (3, 2, 0, 1)
+EARLY_CUT = (0, 960, 1920)
+EXPERT_CUT = (0, 4, 8, 12, 14, 15)
+WEIGHT_CUT = (0, 4, 8, 12, 15)
+STAGE_BUFS = 11
+LOAD_CUT = ((0, 256, 512, 640), (0, 256, 640), (0, 384, 640), (0, 384, 640))
 QUANT_CUT = ((0, 256, 512, 640), (0, 512, 640), (0, 512, 640), (0, 512, 640))
 TOKEN_CUT = (0, 320, 640)
 
@@ -46,6 +47,7 @@ def tile_moe_tk_lin_none_kernel(
     with ExitStack() as ctx:
         lists = ctx.enter_context(tc.tile_pool(name="lists", bufs=1))
         keep = ctx.enter_context(tc.tile_pool(name="keep", bufs=1))
+        stage = ctx.enter_context(tc.tile_pool(name="stage", bufs=STAGE_BUFS))
         psum = ctx.enter_context(tc.psum_pool(name="psum", bufs=1))
 
         slot_token = lists.tile([P, S // LIST_ROWS], U16, name="slot_token")
@@ -53,17 +55,14 @@ def tile_moe_tk_lin_none_kernel(
 
         x_raw = [
             [
-                keep.tile([P, PACK, t1 - t0], F32, name="x_raw%d_%d" % (a, t0), tag="stage%d_%d" % (a, t0), align_bytes=64)
+                stage.tile([P, PACK, t1 - t0], F32, name="x_raw%d_%d" % (a, t0), tag="stage", align_bytes=64)
                 for t0, t1 in spans(LOAD_CUT[a])
             ]
             for a in range(PASSES)
         ]
         x_bf = [keep.tile([P, T, PACK], BF16, name="x_bf%d" % a, align_bytes=64) for a in range(PASSES)]
-        early_words = [keep.tile([P, T], U32, name="early_words%d" % a, align_bytes=64) for a in range(HALF)]
-        late_words = keep.tile([P, HALF * T], U32, name="late_words", align_bytes=64)
-        tok_words = [early_words[0][:], early_words[1][:], late_words[:, 0:T], late_words[:, T : 2 * T]]
-        windows = [early_words[0][:], early_words[1][:], late_words[:, 0:HELD_WINDOW], late_words[:, T : 2 * T]]
-        tok_scales = keep.tile([P, T], U8, name="tok_scales", align_bytes=64)
+        tok_words = keep.tile([P, (PASSES + 1) * T], I32, name="tok_words", align_bytes=64)
+        tok_scales = keep.tile([P, 2 * T], U8, name="tok_scales", align_bytes=64)
         slot_words = [keep.tile([P, S], U32, name="slot_words%d" % a, align_bytes=64) for a in range(PASSES)]
         slot_scales = keep.tile([P, S], U8, name="slot_scales", align_bytes=64)
         last_scales = keep.tile([P, S], U8, name="last_scales", align_bytes=64)
@@ -75,6 +74,7 @@ def tile_moe_tk_lin_none_kernel(
 
         for plane in (w_scales, tok_scales, last_scales):
             nc.vector.memset(plane[:].bitcast(I32), 0)
+        nc.vector.memset(tok_words[:, PASSES * T :], 0)
 
         for a in range(PASSES):
             rows = xT[a * K_PASS : (a + 1) * K_PASS, :].rearrange("(p j) t -> p j t", j=PACK)
@@ -102,7 +102,7 @@ def tile_moe_tk_lin_none_kernel(
         def quantize_tokens(a, piece):
             t0, t1 = spans(QUANT_CUT[a])[piece]
             nc.vector.quantize_mx(
-                out=tok_words[a][:, t0:t1].bitcast(FP8X4),
+                out=tok_words[:, WORD_PLACE[a] * T + t0 : WORD_PLACE[a] * T + t1].bitcast(FP8X4),
                 scales=tok_scales[PLANE_ROW[a] : P, t0:t1],
                 in_=x_bf[a][:, t0:t1, :].rearrange("p t j -> p (t j)"),
             )
@@ -110,6 +110,11 @@ def tile_moe_tk_lin_none_kernel(
         def gather(dst, window, s0, s1):
             offsets = slot_token[:, s0 // LIST_ROWS : s1 // LIST_ROWS]
             nc.vector.tensor_copy(dst[:, s0:s1], window.indirect(offsets))
+
+        def gather_words(a, s0, s1):
+            first = WORD_PLACE[a] * T
+            width = min(2 * T, 8 * (s1 - s0))
+            gather(slot_words[a], tok_words[:, first : first + width].bitcast(U32), s0, s1)
 
         round_tokens(0, 0)
         quantize_tokens(0, 0)
@@ -121,7 +126,6 @@ def tile_moe_tk_lin_none_kernel(
             for piece in range(len(x_raw[a])):
                 round_tokens(a, piece)
 
-        stage_tags = ["stage%d_%d" % (a, t0) for a in range(PASSES) for t0, t1 in spans(LOAD_CUT[a])]
         w8_src = w8_words.rearrange("e a p n t -> p (e a) (n t)").bitcast(I32)
         w4_src = w4_words.rearrange("e a p b -> p (e a) b").bitcast(I32)
         w8, w4 = {}, {}
@@ -129,8 +133,8 @@ def tile_moe_tk_lin_none_kernel(
         def load_weights(g):
             e0, e1 = spans(WEIGHT_CUT)[g]
             rows = slice(HALF * e0, HALF * e1)
-            w8_tile = keep.tile([P, HALF * (e1 - e0), N * 4], U8, name="w8_%d" % g, tag=stage_tags[2 * g], align_bytes=64)
-            w4_tile = keep.tile([P, HALF * (e1 - e0), N * 2], U8, name="w4_%d" % g, tag=stage_tags[2 * g + 1], align_bytes=64)
+            w8_tile = stage.tile([P, HALF * (e1 - e0), N * 4], U8, name="w8_%d" % g, tag="stage", align_bytes=64)
+            w4_tile = stage.tile([P, HALF * (e1 - e0), N * 2], U8, name="w4_%d" % g, tag="stage", align_bytes=64)
             nc.sync.dma_start(w8_tile[:].bitcast(I32), w8_src[:, rows, :])
             nc.sync.dma_start(w4_tile[:].bitcast(I32), w4_src[:, rows, :])
             for m in range(HALF * e0, HALF * e1):
@@ -138,33 +142,32 @@ def tile_moe_tk_lin_none_kernel(
                 w4[m] = w4_tile[:, m - HALF * e0, :].bitcast(FP4X4)
 
         load_weights(0)
-        load_weights(1)
 
         for a in range(HALF):
             for s0, s1 in spans(EARLY_CUT):
-                if s1 == S:
-                    for piece in range(2):
-                        quantize_tokens(a + 1, piece)
-                gather(slot_words[a], windows[a], s0, s1)
+                gather_words(a, s0, s1)
+            for piece in range(2):
+                quantize_tokens(a + 1, piece)
         for piece in range(2):
             quantize_tokens(PASSES - 1, piece)
 
         def gather_scales(half):
-            cut = EARLY_CUT[2 * half : 2 * half + 3]
-            for s0, s1 in spans(cut):
-                gather(slot_scales, tok_scales[:], s0, s1)
-            cols = slice(cut[0] // 4, cut[-1] // 4)
+            s0, s1 = spans(EARLY_CUT)[half]
+            gather(slot_scales, tok_scales[:], s0, s1)
+            cols = slice(s0 // 4, s1 // 4)
             row = PLANE_ROW[PASSES - 1]
             nc.sync.dma_start(last_scales[:].bitcast(I32)[0 : P - row, cols], slot_scales[:].bitcast(I32)[row:P, cols])
 
         for half in range(2):
             gather_scales(half)
-        load_weights(2)
-        gates = keep.tile([P, TOP, T], F32, name="gates", tag=stage_tags[-2], align_bytes=64)
-        nc.sync.dma_start(gates[:], gate.rearrange("r n t -> n r t"))
+            load_weights(1 + half)
+        load_weights(3)
+        gates = [stage.tile([P, T], F32, name="gates%d" % r, tag="stage", align_bytes=64) for r in range(TOP)]
+        for r in range(TOP):
+            nc.sync.dma_start(gates[r][:], gate[r])
         for e0, e1 in spans(EXPERT_CUT):
             for a in range(HALF, PASSES):
-                gather(slot_words[a], windows[a], e0 * C, e1 * C)
+                gather_words(a, e0 * C, e1 * C)
             bank = psum.tile([P, (e1 - e0) * C], F32, name="bank%d" % e0)
             for e in range(e0, e1):
                 slots = slice(e * C, (e + 1) * C)
@@ -189,10 +192,10 @@ def tile_moe_tk_lin_none_kernel(
                     )
             nc.scalar.copy(y[:, e0 * C : e1 * C], bank[:])
 
+        for r in range(TOP):
+            nc.vector.tensor_tensor(terms[r][:], y[:].indirect(token_slot[r][:]), gates[r][:], MULT)
         for t0, t1 in spans(TOKEN_CUT):
-            for r in range(TOP):
-                offsets = token_slot[r][:, t0 // LIST_ROWS : t1 // LIST_ROWS]
-                nc.vector.tensor_tensor(terms[r][:, t0:t1], y[:].indirect(offsets), gates[:, r, t0:t1], MULT)
             nc.vector.tensor_tensor(partial[:, t0:t1], terms[0][:, t0:t1], terms[1][:, t0:t1], ADD)
+        for t0, t1 in spans(TOKEN_CUT):
             nc.vector.tensor_tensor(result[:, t0:t1], partial[:, t0:t1], terms[2][:, t0:t1], ADD)
             nc.sync.dma_start(out[:, t0:t1], result[:, t0:t1])

@@ -28,11 +28,15 @@ PLANE_ROW = (4, 12, 0, 8)
 W8_ROW = 4
 WORD_PLACE = (3, 2, 0, 1)
 EARLY_CUT = (0, 960, 1920)
-EXPERT_CUT = (0, 4, 8, 12, 14, 15)
+EXPERT_CUT = (0, 3, 7, 11, 13, 14, 15)
+FILLER = EXPERT_CUT[1] * C
 WEIGHT_CUT = (0, 4, 8, 12, 15)
 STAGE_BUFS = 11
 LOAD_CUT = ((0, 256, 512, 640), (0, 256, 640), (0, 384, 640), (0, 384, 640))
 QUANT_CUT = ((0, 256, 512, 640), (0, 512, 640), (0, 512, 640), (0, 512, 640))
+SCALE_CUT = (0, 7, 15)
+SCALE_WINDOW = 1408
+SUM_ORDER = (3, 0, 1, 2)
 TOKEN_CUT = (0, 320, 640)
 
 
@@ -62,17 +66,21 @@ def tile_moe_tk_lin_none_kernel(
         ]
         x_bf = [keep.tile([P, T, PACK], BF16, name="x_bf%d" % a, align_bytes=64) for a in range(PASSES)]
         tok_words = keep.tile([P, (PASSES + 1) * T], I32, name="tok_words", align_bytes=64)
-        tok_scales = keep.tile([P, 2 * T], U8, name="tok_scales", align_bytes=64)
+        tok_scales = keep.tile([P, SCALE_WINDOW], U8, name="tok_scales", align_bytes=64)
         slot_words = [keep.tile([P, S], U32, name="slot_words%d" % a, align_bytes=64) for a in range(PASSES)]
-        slot_scales = keep.tile([P, S], U8, name="slot_scales", align_bytes=64)
-        last_scales = keep.tile([P, S], U8, name="last_scales", align_bytes=64)
+        slot_scales = [
+            keep.tile([P, (e1 - e0) * C], U8, name="slot_scales%d" % e0, align_bytes=64) for e0, e1 in spans(SCALE_CUT)
+        ]
+        last_scales = [
+            keep.tile([P, (e1 - e0) * C], U8, name="last_scales%d" % e0, align_bytes=64) for e0, e1 in spans(SCALE_CUT)
+        ]
         w_scales = keep.tile([P, E * HALF * N], U8, name="w_scales", align_bytes=64)
         y = keep.tile([P, S], F32, name="y")
         terms = [keep.tile([P, T], F32, name="term%d" % r) for r in range(TOP)]
         partial = keep.tile([P, T], F32, name="partial")
         result = keep.tile([P, T], F32, name="result")
 
-        for plane in (w_scales, tok_scales, last_scales):
+        for plane in [w_scales, tok_scales] + last_scales:
             nc.vector.memset(plane[:].bitcast(I32), 0)
         nc.vector.memset(tok_words[:, PASSES * T :], 0)
 
@@ -86,9 +94,7 @@ def tile_moe_tk_lin_none_kernel(
             nc.sync.dma_start(tile[:], pos)
         dst = w_scales[:].bitcast(I32).rearrange("p (m n) -> p m n", n=N // 4)
         for row, scales in ((W8_ROW, w8_scales), (0, w4_scales)):
-            src = scales.bitcast(I32).rearrange("e a (q r) n -> r q (e a) n", r=4)
-            for r in range(4):
-                nc.sync.dma_start(dst[row + r : P : 32], src[r])
+            nc.sync.dma_start(dst[row:P:8], scales.bitcast(I32).rearrange("e a q n -> q (e a) n"))
 
         def round_tokens(a, piece):
             t0, t1 = spans(LOAD_CUT[a])[piece]
@@ -109,12 +115,12 @@ def tile_moe_tk_lin_none_kernel(
 
         def gather(dst, window, s0, s1):
             offsets = slot_token[:, s0 // LIST_ROWS : s1 // LIST_ROWS]
-            nc.vector.tensor_copy(dst[:, s0:s1], window.indirect(offsets))
+            nc.vector.tensor_copy(dst, window.indirect(offsets))
 
         def gather_words(a, s0, s1):
             first = WORD_PLACE[a] * T
-            width = min(2 * T, 8 * (s1 - s0))
-            gather(slot_words[a], tok_words[:, first : first + width].bitcast(U32), s0, s1)
+            width = T if (a, s1) == (HALF, FILLER) else min(2 * T, 8 * (s1 - s0))
+            gather(slot_words[a][:, s0:s1], tok_words[:, first : first + width].bitcast(U32), s0, s1)
 
         round_tokens(0, 0)
         quantize_tokens(0, 0)
@@ -142,53 +148,63 @@ def tile_moe_tk_lin_none_kernel(
                 w4[m] = w4_tile[:, m - HALF * e0, :].bitcast(FP4X4)
 
         load_weights(0)
+        scale_words = w_scales[:].bitcast(I32)
+        for row in (W8_ROW, 0):
+            for r in range(1, 4):
+                nc.sync.dma_start(scale_words[row + r : P : 32, :], scale_words[row + 8 * r : P : 32, :])
+        load_weights(1)
 
         for a in range(HALF):
             for s0, s1 in spans(EARLY_CUT):
                 gather_words(a, s0, s1)
             for piece in range(2):
                 quantize_tokens(a + 1, piece)
+        gather_words(HALF, 0, FILLER)
         for piece in range(2):
             quantize_tokens(PASSES - 1, piece)
 
         def gather_scales(half):
-            s0, s1 = spans(EARLY_CUT)[half]
-            gather(slot_scales, tok_scales[:], s0, s1)
-            cols = slice(s0 // 4, s1 // 4)
+            e0, e1 = spans(SCALE_CUT)[half]
+            gather(slot_scales[half][:], tok_scales[:], e0 * C, e1 * C)
             row = PLANE_ROW[PASSES - 1]
-            nc.sync.dma_start(last_scales[:].bitcast(I32)[0 : P - row, cols], slot_scales[:].bitcast(I32)[row:P, cols])
+            for p0, p1 in ((0, 64), (64, 68), (96, 100)):
+                nc.sync.dma_start(
+                    last_scales[half][p0:p1, :].bitcast(I32), slot_scales[half][row + p0 : row + p1, :].bitcast(I32)
+                )
 
         for half in range(2):
             gather_scales(half)
-            load_weights(1 + half)
-        load_weights(3)
+            load_weights(2 + half)
         gates = [stage.tile([P, T], F32, name="gates%d" % r, tag="stage", align_bytes=64) for r in range(TOP)]
         for r in range(TOP):
             nc.sync.dma_start(gates[r][:], gate[r])
         for e0, e1 in spans(EXPERT_CUT):
-            for a in range(HALF, PASSES):
-                gather_words(a, e0 * C, e1 * C)
+            gather_words(PASSES - 1, e0 * C, e1 * C)
+            if e0 > 0:
+                gather_words(HALF, e0 * C, e1 * C)
             bank = psum.tile([P, (e1 - e0) * C], F32, name="bank%d" % e0)
             for e in range(e0, e1):
                 slots = slice(e * C, (e + 1) * C)
-                for a in range(PASSES):
+                half = 0 if e < SCALE_CUT[1] else 1
+                part = slice((e - SCALE_CUT[half]) * C, (e - SCALE_CUT[half] + 1) * C)
+                for a in SUM_ORDER:
                     m = HALF * e + a % HALF
                     if a < HALF:
                         weights, w_row = w8[m], W8_ROW
                     else:
                         weights, w_row = w4[m], 0
                     if a == PASSES - 1:
-                        x_plane = last_scales[:, slots]
+                        x_plane = last_scales[half][:, part]
                     else:
-                        x_plane = slot_scales[PLANE_ROW[a] : P, slots]
+                        x_plane = slot_scales[half][PLANE_ROW[a] : P, part]
                     nc.tensor.matmul_mx(
                         out=bank[:, (e - e0) * C : (e - e0 + 1) * C],
                         lhsT=weights,
                         lhsT_scale=w_scales[w_row:P, m * N : (m + 1) * N],
                         rhs=slot_words[a][:, slots].bitcast(FP8X4),
                         rhs_scale=x_plane,
-                        start=(a == 0),
-                        stop=(a == PASSES - 1),
+                        start=(a == SUM_ORDER[0]),
+                        stop=(a == SUM_ORDER[-1]),
                     )
             nc.scalar.copy(y[:, e0 * C : e1 * C], bank[:])
 

@@ -27,17 +27,22 @@ LIST_ROWS = 16
 PLANE_ROW = (4, 12, 0, 8)
 W8_ROW = 4
 WORD_PLACE = (3, 2, 0, 1)
-EARLY_CUT = (0, 960, 1920)
-EXPERT_CUT = (0, 3, 7, 11, 13, 14, 15)
-FILLER = EXPERT_CUT[1] * C
+EARLY_CUT = (0, 768, 1536, 1920)
+OPEN_CUT = (0, 3, 7, 11, 15)
+CLOSE_CUT = (0, 3, 7, 11, 13, 14, 15)
+BANKS = 8
+FILLER = CLOSE_CUT[1] * C
+FILLER_CUT = (0, 256, FILLER)
 WEIGHT_CUT = (0, 4, 8, 12, 15)
-STAGE_BUFS = 11
-LOAD_CUT = ((0, 256, 512, 640), (0, 256, 640), (0, 384, 640), (0, 384, 640))
+STAGE_BUFS = 9
+LOAD_CUT = ((0, 256, 512, 640), (0, 256, 512, 640), (0, 384, 640), (0, 384, 640))
 QUANT_CUT = ((0, 256, 512, 640), (0, 512, 640), (0, 512, 640), (0, 512, 640))
 SCALE_CUT = (0, 7, 15)
 SCALE_WINDOW = 1408
 SUM_ORDER = (3, 0, 1, 2)
 TOKEN_CUT = (0, 320, 640)
+STORE_CUT = (0, 256, 512, 640)
+VECTOR_SHARE = (256, 256, 128)
 
 
 def spans(cut):
@@ -59,7 +64,9 @@ def tile_moe_tk_lin_none_kernel(
 
         x_raw = [
             [
-                stage.tile([P, PACK, t1 - t0], F32, name="x_raw%d_%d" % (a, t0), tag="stage", align_bytes=64)
+                keep.tile([P, PACK, t1 - t0], F32, name="x_last%d" % a, tag="hold%d" % a, align_bytes=64)
+                if a > 0 and t1 == T
+                else stage.tile([P, PACK, t1 - t0], F32, name="x_raw%d_%d" % (a, t0), tag="stage", align_bytes=64)
                 for t0, t1 in spans(LOAD_CUT[a])
             ]
             for a in range(PASSES)
@@ -67,7 +74,7 @@ def tile_moe_tk_lin_none_kernel(
         x_bf = [keep.tile([P, T, PACK], BF16, name="x_bf%d" % a, align_bytes=64) for a in range(PASSES)]
         tok_words = keep.tile([P, (PASSES + 1) * T], I32, name="tok_words", align_bytes=64)
         tok_scales = keep.tile([P, SCALE_WINDOW], U8, name="tok_scales", align_bytes=64)
-        slot_words = [keep.tile([P, S], U32, name="slot_words%d" % a, align_bytes=64) for a in range(PASSES)]
+        slot_words = {}
         slot_scales = [
             keep.tile([P, (e1 - e0) * C], U8, name="slot_scales%d" % e0, align_bytes=64) for e0, e1 in spans(SCALE_CUT)
         ]
@@ -98,12 +105,11 @@ def tile_moe_tk_lin_none_kernel(
 
         def round_tokens(a, piece):
             t0, t1 = spans(LOAD_CUT[a])[piece]
-            dst = x_bf[a][:, t0:t1, :].rearrange("p (c i) j -> p c j i", i=4)
-            src = x_raw[a][piece][:].rearrange("p j (c i) -> p c j i", i=4)
-            if a == 0:
-                nc.vector.tensor_copy(dst, src)
-            else:
-                nc.scalar.copy(dst, src)
+            split = VECTOR_SHARE[piece] if a == 0 else 0
+            for copy, c0, c1 in ((nc.vector.tensor_copy, 0, split), (nc.scalar.copy, split, t1 - t0)):
+                if c1 > c0:
+                    dst = x_bf[a][:, t0 + c0 : t0 + c1, :].rearrange("p (c i) j -> p c j i", i=4)
+                    copy(dst, x_raw[a][piece][:, :, c0:c1].rearrange("p j (c i) -> p c j i", i=4))
 
         def quantize_tokens(a, piece):
             t0, t1 = spans(QUANT_CUT[a])[piece]
@@ -117,10 +123,14 @@ def tile_moe_tk_lin_none_kernel(
             offsets = slot_token[:, s0 // LIST_ROWS : s1 // LIST_ROWS]
             nc.vector.tensor_copy(dst, window.indirect(offsets))
 
-        def gather_words(a, s0, s1):
+        def gather_words(a, s0, s1, held=False):
             first = WORD_PLACE[a] * T
-            width = T if (a, s1) == (HALF, FILLER) else min(2 * T, 8 * (s1 - s0))
-            gather(slot_words[a][:, s0:s1], tok_words[:, first : first + width].bitcast(U32), s0, s1)
+            width = T if a == HALF and s1 <= FILLER else min(2 * T, 8 * (s1 - s0))
+            name = "slot_words%d_%d" % (a, s0)
+            words = keep.tile([P, s1 - s0], U32, name=name, tag="hold%d" % (a + 1) if held else name, align_bytes=64)
+            gather(words[:], tok_words[:, first : first + width].bitcast(U32), s0, s1)
+            for s in range(s0, s1, C):
+                slot_words[a, s // C] = words[:, s - s0 : s - s0 + C].bitcast(FP8X4)
 
         round_tokens(0, 0)
         quantize_tokens(0, 0)
@@ -154,14 +164,12 @@ def tile_moe_tk_lin_none_kernel(
                 nc.sync.dma_start(scale_words[row + r : P : 32, :], scale_words[row + 8 * r : P : 32, :])
         load_weights(1)
 
-        for a in range(HALF):
-            for s0, s1 in spans(EARLY_CUT):
+        for a, cut in enumerate((EARLY_CUT, EARLY_CUT, FILLER_CUT)):
+            for s0, s1 in spans(cut)[:-1]:
                 gather_words(a, s0, s1)
             for piece in range(2):
                 quantize_tokens(a + 1, piece)
-        gather_words(HALF, 0, FILLER)
-        for piece in range(2):
-            quantize_tokens(PASSES - 1, piece)
+            gather_words(a, cut[-2], cut[-1], held=True)
 
         def gather_scales(half):
             e0, e1 = spans(SCALE_CUT)[half]
@@ -172,46 +180,66 @@ def tile_moe_tk_lin_none_kernel(
                     last_scales[half][p0:p1, :].bitcast(I32), slot_scales[half][row + p0 : row + p1, :].bitcast(I32)
                 )
 
-        for half in range(2):
-            gather_scales(half)
-            load_weights(2 + half)
-        gates = [stage.tile([P, T], F32, name="gates%d" % r, tag="stage", align_bytes=64) for r in range(TOP)]
-        for r in range(TOP):
-            nc.sync.dma_start(gates[r][:], gate[r])
-        for e0, e1 in spans(EXPERT_CUT):
-            gather_words(PASSES - 1, e0 * C, e1 * C)
-            if e0 > 0:
-                gather_words(HALF, e0 * C, e1 * C)
-            bank = psum.tile([P, (e1 - e0) * C], F32, name="bank%d" % e0)
+        gather_scales(0)
+        load_weights(2)
+        load_weights(3)
+        gather_scales(1)
+        gates = stage.tile([P, TOP, T], F32, name="gates", tag="stage", align_bytes=64)
+        nc.sync.dma_start(gates[:], gate.rearrange("r n t -> n r t"))
+        sums = {}
+
+        def multiply(e, passes):
+            half = 0 if e < SCALE_CUT[1] else 1
+            part = slice((e - SCALE_CUT[half]) * C, (e - SCALE_CUT[half] + 1) * C)
+            for a in passes:
+                m = HALF * e + a % HALF
+                if a < HALF:
+                    weights, w_row = w8[m], W8_ROW
+                else:
+                    weights, w_row = w4[m], 0
+                if a == PASSES - 1:
+                    x_plane = last_scales[half][:, part]
+                else:
+                    x_plane = slot_scales[half][PLANE_ROW[a] : P, part]
+                nc.tensor.matmul_mx(
+                    out=sums[e][:],
+                    lhsT=weights,
+                    lhsT_scale=w_scales[w_row:P, m * N : (m + 1) * N],
+                    rhs=slot_words[a, e],
+                    rhs_scale=x_plane,
+                    start=(a == SUM_ORDER[0]),
+                    stop=(a == SUM_ORDER[-1]),
+                )
+
+        def open_sums(e0, e1):
             for e in range(e0, e1):
-                slots = slice(e * C, (e + 1) * C)
-                half = 0 if e < SCALE_CUT[1] else 1
-                part = slice((e - SCALE_CUT[half]) * C, (e - SCALE_CUT[half] + 1) * C)
-                for a in SUM_ORDER:
-                    m = HALF * e + a % HALF
-                    if a < HALF:
-                        weights, w_row = w8[m], W8_ROW
-                    else:
-                        weights, w_row = w4[m], 0
-                    if a == PASSES - 1:
-                        x_plane = last_scales[half][:, part]
-                    else:
-                        x_plane = slot_scales[half][PLANE_ROW[a] : P, part]
-                    nc.tensor.matmul_mx(
-                        out=bank[:, (e - e0) * C : (e - e0 + 1) * C],
-                        lhsT=weights,
-                        lhsT_scale=w_scales[w_row:P, m * N : (m + 1) * N],
-                        rhs=slot_words[a][:, slots].bitcast(FP8X4),
-                        rhs_scale=x_plane,
-                        start=(a == SUM_ORDER[0]),
-                        stop=(a == SUM_ORDER[-1]),
-                    )
-            nc.scalar.copy(y[:, e0 * C : e1 * C], bank[:])
+                sums[e] = psum.tile([P, C], F32, name="sums%d" % e, tag="bank%d" % (e % BANKS))
+                multiply(e, SUM_ORDER[:-1])
+
+        def close_sums(e0, e1):
+            for e in range(e0, e1):
+                multiply(e, SUM_ORDER[-1:])
+                nc.scalar.copy(y[:, e * C : (e + 1) * C], sums[e][:])
+
+        opens, closes = spans(OPEN_CUT), spans(CLOSE_CUT)
+        gather_words(PASSES - 1, opens[0][0] * C, opens[0][1] * C)
+        open_sums(*opens[0])
+        close_sums(*closes[0])
+        gather_words(PASSES - 1, opens[1][0] * C, opens[1][1] * C)
+        open_sums(*opens[1])
+        for (o0, o1), (c0, c1) in zip(opens[2:], closes[1:]):
+            gather_words(PASSES - 1, o0 * C, o1 * C)
+            open_sums(o0, o1)
+            gather_words(HALF, c0 * C, c1 * C)
+            close_sums(c0, c1)
+        for c0, c1 in closes[len(opens) - 1 :]:
+            gather_words(HALF, c0 * C, c1 * C)
+            close_sums(c0, c1)
 
         for r in range(TOP):
-            nc.vector.tensor_tensor(terms[r][:], y[:].indirect(token_slot[r][:]), gates[r][:], MULT)
+            nc.vector.tensor_tensor(terms[r][:], y[:].indirect(token_slot[r][:]), gates[:, r, :], MULT)
         for t0, t1 in spans(TOKEN_CUT):
             nc.vector.tensor_tensor(partial[:, t0:t1], terms[0][:, t0:t1], terms[1][:, t0:t1], ADD)
-        for t0, t1 in spans(TOKEN_CUT):
+        for t0, t1 in spans(STORE_CUT):
             nc.vector.tensor_tensor(result[:, t0:t1], partial[:, t0:t1], terms[2][:, t0:t1], ADD)
             nc.sync.dma_start(out[:, t0:t1], result[:, t0:t1])

@@ -27,13 +27,12 @@ LIST_ROWS = 16
 PLANE_ROW = (4, 12, 0, 8)
 W8_ROW = 4
 WORD_PLACE = (3, 2, 0, 1)
-EARLY_CUT = (0, 768, 1536, 1920)
+EARLY_CUT = (0, 896, 1792, 1920)
 OPEN_CUT = (0, 3, 7, 11, 15)
 CLOSE_CUT = (0, 3, 7, 11, 13, 14, 15)
 BANKS = 8
 FILLER = CLOSE_CUT[1] * C
 FILLER_CUT = (0, 256, FILLER)
-WEIGHT_CUT = (0, 4, 8, 12, 15)
 STAGE_BUFS = 9
 LOAD_CUT = ((0, 256, 512, 640), (0, 256, 512, 640), (0, 384, 640), (0, 384, 640))
 QUANT_CUT = ((0, 256, 512, 640), (0, 512, 640), (0, 512, 640), (0, 512, 640))
@@ -142,27 +141,28 @@ def tile_moe_tk_lin_none_kernel(
             for piece in range(len(x_raw[a])):
                 round_tokens(a, piece)
 
-        w8_src = w8_words.rearrange("e a p n t -> p (e a) (n t)").bitcast(I32)
-        w4_src = w4_words.rearrange("e a p b -> p (e a) b").bitcast(I32)
-        w8, w4 = {}, {}
+        w8_src = w8_words.rearrange("e a p n t -> p e a (n t)").bitcast(I32)
+        w4_src = w4_words.rearrange("e a p b -> p e a b").bitcast(I32)
+        weights = {}
 
-        def load_weights(g):
-            e0, e1 = spans(WEIGHT_CUT)[g]
-            rows = slice(HALF * e0, HALF * e1)
-            w8_tile = stage.tile([P, HALF * (e1 - e0), N * 4], U8, name="w8_%d" % g, tag="stage", align_bytes=64)
-            w4_tile = stage.tile([P, HALF * (e1 - e0), N * 2], U8, name="w4_%d" % g, tag="stage", align_bytes=64)
-            nc.sync.dma_start(w8_tile[:].bitcast(I32), w8_src[:, rows, :])
-            nc.sync.dma_start(w4_tile[:].bitcast(I32), w4_src[:, rows, :])
-            for m in range(HALF * e0, HALF * e1):
-                w8[m] = w8_tile[:, m - HALF * e0, :].bitcast(FP8X4)
-                w4[m] = w4_tile[:, m - HALF * e0, :].bitcast(FP4X4)
+        def load_weights(e0, e1, a0, a1):
+            src, width, dtype = (w8_src, 4, FP8X4) if a0 < HALF else (w4_src, 2, FP4X4)
+            tile = stage.tile(
+                [P, e1 - e0, a1 - a0, N * width], U8, name="w%d_%d" % (e0, a0), tag="stage", align_bytes=64
+            )
+            nc.sync.dma_start(tile[:].bitcast(I32), src[:, e0:e1, a0 % HALF : (a1 - 1) % HALF + 1, :])
+            for e in range(e0, e1):
+                for a in range(a0, a1):
+                    weights[e, a] = tile[:, e - e0, a - a0, :].bitcast(dtype)
 
-        load_weights(0)
+        load_weights(0, 3, 0, 2)
+        load_weights(0, 3, 2, 4)
         scale_words = w_scales[:].bitcast(I32)
         for row in (W8_ROW, 0):
             for r in range(1, 4):
                 nc.sync.dma_start(scale_words[row + r : P : 32, :], scale_words[row + 8 * r : P : 32, :])
-        load_weights(1)
+        load_weights(3, 7, 0, 2)
+        load_weights(3, 7, 2, 4)
 
         for a, cut in enumerate((EARLY_CUT, EARLY_CUT, FILLER_CUT)):
             for s0, s1 in spans(cut)[:-1]:
@@ -181,9 +181,11 @@ def tile_moe_tk_lin_none_kernel(
                 )
 
         gather_scales(0)
-        load_weights(2)
-        load_weights(3)
+        load_weights(7, 11, 0, 2)
+        load_weights(7, 15, 3, 4)
         gather_scales(1)
+        load_weights(11, 15, 0, 2)
+        load_weights(7, 15, 2, 3)
         gates = stage.tile([P, TOP, T], F32, name="gates", tag="stage", align_bytes=64)
         nc.sync.dma_start(gates[:], gate.rearrange("r n t -> n r t"))
         sums = {}
@@ -193,17 +195,14 @@ def tile_moe_tk_lin_none_kernel(
             part = slice((e - SCALE_CUT[half]) * C, (e - SCALE_CUT[half] + 1) * C)
             for a in passes:
                 m = HALF * e + a % HALF
-                if a < HALF:
-                    weights, w_row = w8[m], W8_ROW
-                else:
-                    weights, w_row = w4[m], 0
+                w_row = W8_ROW if a < HALF else 0
                 if a == PASSES - 1:
                     x_plane = last_scales[half][:, part]
                 else:
                     x_plane = slot_scales[half][PLANE_ROW[a] : P, part]
                 nc.tensor.matmul_mx(
                     out=sums[e][:],
-                    lhsT=weights,
+                    lhsT=weights[e, a],
                     lhsT_scale=w_scales[w_row:P, m * N : (m + 1) * N],
                     rhs=slot_words[a, e],
                     rhs_scale=x_plane,

@@ -1,6 +1,7 @@
 from contextlib import ExitStack
 
 import concourse.mybir as mybir
+from concourse.masks import make_identity
 
 K, T, E, C, N = 2048, 640, 15, 128, 128
 TOP = 3
@@ -31,9 +32,11 @@ EARLY_CUT = (0, 896, 1792, 1920)
 OPEN_CUT = (0, 3, 7, 11, 15)
 CLOSE_CUT = (0, 3, 7, 11, 13, 14, 15)
 BANKS = 8
+CHUNKS = T // P
+BANK = 512
 FILLER = CLOSE_CUT[1] * C
 FILLER_CUT = (0, 256, FILLER)
-STAGE_BUFS = 9
+STAGE_BUFS = 8
 LOAD_CUT = ((0, 256, 512, 640), (0, 256, 512, 640), (0, 384, 640), (0, 384, 640))
 QUANT_CUT = ((0, 256, 512, 640), (0, 512, 640), (0, 512, 640), (0, 512, 640))
 SCALE_CUT = (0, 7, 15)
@@ -65,6 +68,8 @@ def tile_moe_tk_lin_none_kernel(
             [
                 keep.tile([P, PACK, t1 - t0], F32, name="x_last%d" % a, tag="hold%d" % a, align_bytes=64)
                 if a > 0 and t1 == T
+                else keep.tile([P, PACK, t1 - t0], F32, name="x_late", tag="gates", align_bytes=64)
+                if a == PASSES - 1
                 else stage.tile([P, PACK, t1 - t0], F32, name="x_raw%d_%d" % (a, t0), tag="stage", align_bytes=64)
                 for t0, t1 in spans(LOAD_CUT[a])
             ]
@@ -86,6 +91,12 @@ def tile_moe_tk_lin_none_kernel(
         partial = keep.tile([P, T], F32, name="partial")
         result = keep.tile([P, T], F32, name="result")
 
+        identity = keep.tile([P, P], F32, name="identity")
+        gate_rows = keep.tile([P, P], F32, name="gate_rows")
+        gate_cols = keep.tile([P, TOP * CHUNKS], F32, name="gate_cols")
+        make_identity(nc, identity[:])
+        nc.vector.memset(gate_rows[:], 0.0)
+        nc.scalar.dma_start(gate_rows[: TOP * CHUNKS, :], gate.rearrange("r n (c t) -> (r n c) t", t=P)[::P, :])
         for plane in [w_scales, tok_scales] + last_scales:
             nc.vector.memset(plane[:].bitcast(I32), 0)
         nc.vector.memset(tok_words[:, PASSES * T :], 0)
@@ -141,6 +152,21 @@ def tile_moe_tk_lin_none_kernel(
             for piece in range(len(x_raw[a])):
                 round_tokens(a, piece)
 
+        turned = psum.tile([P, P], F32, name="turned", tag="bank3")
+        nc.tensor.transpose(turned[:], gate_rows[:], identity[:])
+        nc.scalar.copy(gate_cols[:], turned[:, : TOP * CHUNKS])
+        gates = keep.tile([P, TOP * T], F32, name="gates", tag="gates", align_bytes=64)
+        for b, t0 in enumerate(range(0, TOP * T, BANK)):
+            t1 = min(t0 + BANK, TOP * T)
+            spread = psum.tile([P, t1 - t0], F32, name="spread%d" % b, tag="bank%d" % (4 + b))
+            for t in range(t0, t1, P):
+                r, c = divmod(t // P, CHUNKS)
+                col = r * CHUNKS + 2 * c % CHUNKS
+                nc.tensor.transpose(
+                    spread[:, t - t0 : t - t0 + P], gate_cols[:, col : col + 1].to_broadcast([P, P]), identity[:]
+                )
+            nc.scalar.copy(gates[:, t0:t1], spread[:])
+
         w8_src = w8_words.rearrange("e a p n t -> p e a (n t)").bitcast(I32)
         w4_src = w4_words.rearrange("e a p b -> p e a b").bitcast(I32)
         weights = {}
@@ -186,8 +212,6 @@ def tile_moe_tk_lin_none_kernel(
         gather_scales(1)
         load_weights(11, 15, 0, 2)
         load_weights(7, 15, 2, 3)
-        gates = stage.tile([P, TOP, T], F32, name="gates", tag="stage", align_bytes=64)
-        nc.sync.dma_start(gates[:], gate.rearrange("r n t -> n r t"))
         sums = {}
 
         def multiply(e, passes):
@@ -236,7 +260,7 @@ def tile_moe_tk_lin_none_kernel(
             close_sums(c0, c1)
 
         for r in range(TOP):
-            nc.vector.tensor_tensor(terms[r][:], y[:].indirect(token_slot[r][:]), gates[:, r, :], MULT)
+            nc.vector.tensor_tensor(terms[r][:], y[:].indirect(token_slot[r][:]), gates[:, r * T : (r + 1) * T], MULT)
         for t0, t1 in spans(TOKEN_CUT):
             nc.vector.tensor_tensor(partial[:, t0:t1], terms[0][:, t0:t1], terms[1][:, t0:t1], ADD)
         for t0, t1 in spans(STORE_CUT):

@@ -34,6 +34,7 @@ CLOSE_CUT = (0, 3, 7, 11, 13, 14, 15)
 BANKS = 8
 CHUNKS = T // P
 BANK = 512
+ALIGN = 256
 FILLER = CLOSE_CUT[1] * C
 FILLER_CUT = (0, 256, FILLER)
 STAGE_BUFS = 8
@@ -66,34 +67,34 @@ def tile_moe_tk_lin_none_kernel(
 
         x_raw = [
             [
-                keep.tile([P, PACK, t1 - t0], F32, name="x_last%d" % a, tag="hold%d" % a, align_bytes=64)
+                keep.tile([P, PACK, t1 - t0], F32, name="x_last%d" % a, tag="hold%d" % a, align_bytes=ALIGN)
                 if a > 0 and t1 == T
-                else keep.tile([P, PACK, t1 - t0], F32, name="x_late", tag="gates", align_bytes=64)
+                else keep.tile([P, PACK, t1 - t0], F32, name="x_late", tag="gates", align_bytes=ALIGN)
                 if a == PASSES - 1
-                else stage.tile([P, PACK, t1 - t0], F32, name="x_raw%d_%d" % (a, t0), tag="stage", align_bytes=64)
+                else stage.tile([P, PACK, t1 - t0], F32, name="x_raw%d_%d" % (a, t0), tag="stage", align_bytes=ALIGN)
                 for t0, t1 in spans(LOAD_CUT[a])
             ]
             for a in range(PASSES)
         ]
-        x_bf = [keep.tile([P, T, PACK], BF16, name="x_bf%d" % a, align_bytes=64) for a in range(PASSES)]
-        tok_words = keep.tile([P, (PASSES + 1) * T], I32, name="tok_words", align_bytes=64)
-        tok_scales = keep.tile([P, SCALE_WINDOW], U8, name="tok_scales", align_bytes=64)
+        x_bf = [keep.tile([P, T, PACK], BF16, name="x_bf%d" % a, align_bytes=ALIGN) for a in range(PASSES)]
+        tok_words = keep.tile([P, (PASSES + 1) * T], I32, name="tok_words", align_bytes=ALIGN)
+        tok_scales = keep.tile([P, SCALE_WINDOW], U8, name="tok_scales", align_bytes=ALIGN)
         slot_words = {}
         slot_scales = [
-            keep.tile([P, (e1 - e0) * C], U8, name="slot_scales%d" % e0, align_bytes=64) for e0, e1 in spans(SCALE_CUT)
+            keep.tile([P, (e1 - e0) * C], U8, name="slot_scales%d" % e0, align_bytes=ALIGN) for e0, e1 in spans(SCALE_CUT)
         ]
         last_scales = [
-            keep.tile([P, (e1 - e0) * C], U8, name="last_scales%d" % e0, align_bytes=64) for e0, e1 in spans(SCALE_CUT)
+            keep.tile([P, (e1 - e0) * C], U8, name="last_scales%d" % e0, align_bytes=ALIGN) for e0, e1 in spans(SCALE_CUT)
         ]
-        w_scales = keep.tile([P, E * HALF * N], U8, name="w_scales", align_bytes=64)
-        y = keep.tile([P, S], F32, name="y")
-        terms = [keep.tile([P, T], F32, name="term%d" % r) for r in range(TOP)]
-        partial = keep.tile([P, T], F32, name="partial")
-        result = keep.tile([P, T], F32, name="result")
+        w_scales = keep.tile([P, E * HALF * N], U8, name="w_scales", align_bytes=ALIGN)
+        y = keep.tile([P, S], F32, name="y", align_bytes=ALIGN)
+        terms = [keep.tile([P, T], F32, name="term%d" % r, align_bytes=ALIGN) for r in range(TOP)]
+        partial = keep.tile([P, T], F32, name="partial", align_bytes=ALIGN)
+        result = keep.tile([P, T], F32, name="result", align_bytes=ALIGN)
 
-        identity = keep.tile([P, P], F32, name="identity")
-        gate_rows = keep.tile([P, P], F32, name="gate_rows")
-        gate_cols = keep.tile([P, TOP * CHUNKS], F32, name="gate_cols")
+        identity = keep.tile([P, P], F32, name="identity", align_bytes=ALIGN)
+        gate_rows = keep.tile([P, P], F32, name="gate_rows", align_bytes=ALIGN)
+        gate_cols = keep.tile([P, TOP * CHUNKS], F32, name="gate_cols", align_bytes=ALIGN)
         make_identity(nc, identity[:])
         nc.vector.memset(gate_rows[:], 0.0)
         nc.scalar.dma_start(gate_rows[: TOP * CHUNKS, :], gate.rearrange("r n (c t) -> (r n c) t", t=P)[::P, :])
@@ -137,7 +138,7 @@ def tile_moe_tk_lin_none_kernel(
             first = WORD_PLACE[a] * T
             width = T if a == HALF and s1 <= FILLER else min(2 * T, 8 * (s1 - s0))
             name = "slot_words%d_%d" % (a, s0)
-            words = keep.tile([P, s1 - s0], U32, name=name, tag="hold%d" % (a + 1) if held else name, align_bytes=64)
+            words = keep.tile([P, s1 - s0], U32, name=name, tag="hold%d" % (a + 1) if held else name, align_bytes=ALIGN)
             gather(words[:], tok_words[:, first : first + width].bitcast(U32), s0, s1)
             for s in range(s0, s1, C):
                 slot_words[a, s // C] = words[:, s - s0 : s - s0 + C].bitcast(FP8X4)
@@ -155,7 +156,7 @@ def tile_moe_tk_lin_none_kernel(
         turned = psum.tile([P, P], F32, name="turned", tag="bank3")
         nc.tensor.transpose(turned[:], gate_rows[:], identity[:])
         nc.scalar.copy(gate_cols[:], turned[:, : TOP * CHUNKS])
-        gates = keep.tile([P, TOP * T], F32, name="gates", tag="gates", align_bytes=64)
+        gates = keep.tile([P, TOP * T], F32, name="gates", tag="gates", align_bytes=ALIGN)
         for b, t0 in enumerate(range(0, TOP * T, BANK)):
             t1 = min(t0 + BANK, TOP * T)
             spread = psum.tile([P, t1 - t0], F32, name="spread%d" % b, tag="bank%d" % (4 + b))
@@ -174,7 +175,7 @@ def tile_moe_tk_lin_none_kernel(
         def load_weights(e0, e1, a0, a1):
             src, width, dtype = (w8_src, 4, FP8X4) if a0 < HALF else (w4_src, 2, FP4X4)
             tile = stage.tile(
-                [P, e1 - e0, a1 - a0, N * width], U8, name="w%d_%d" % (e0, a0), tag="stage", align_bytes=64
+                [P, e1 - e0, a1 - a0, N * width], U8, name="w%d_%d" % (e0, a0), tag="stage", align_bytes=ALIGN
             )
             nc.sync.dma_start(tile[:].bitcast(I32), src[:, e0:e1, a0 % HALF : (a1 - 1) % HALF + 1, :])
             for e in range(e0, e1):

@@ -43,8 +43,8 @@ QUANT_CUT = ((0, 256, 512, 640), (0, 512, 640), (0, 512, 640), (0, 512, 640))
 SCALE_CUT = (0, 7, 15)
 SCALE_WINDOW = 1408
 SUM_ORDER = (3, 0, 1, 2)
-TOKEN_CUT = (0, 320, 640)
-STORE_CUT = (0, 256, 512, 640)
+TURNED = 384
+STORE_CUT = (TURNED, 512, 640)
 VECTOR_SHARE = (256, 256, 128)
 
 
@@ -88,9 +88,6 @@ def tile_moe_tk_lin_none_kernel(
         ]
         w_scales = keep.tile([P, E * HALF * N], U8, name="w_scales", align_bytes=ALIGN)
         y = keep.tile([P, S], F32, name="y", align_bytes=ALIGN)
-        terms = [keep.tile([P, T], F32, name="term%d" % r, align_bytes=ALIGN) for r in range(TOP)]
-        partial = keep.tile([P, T], F32, name="partial", align_bytes=ALIGN)
-        result = keep.tile([P, T], F32, name="result", align_bytes=ALIGN)
 
         identity = keep.tile([P, P], F32, name="identity", align_bytes=ALIGN)
         gate_rows = keep.tile([P, P], F32, name="gate_rows", align_bytes=ALIGN)
@@ -260,10 +257,40 @@ def tile_moe_tk_lin_none_kernel(
             gather_words(HALF, c0 * C, c1 * C)
             close_sums(c0, c1)
 
+        def gated(r, t0, t1):
+            term = keep.tile([P, t1 - t0], F32, name="term%d_%d" % (r, t0), align_bytes=ALIGN)
+            offsets = token_slot[r][:, t0 // LIST_ROWS : t1 // LIST_ROWS]
+            nc.vector.tensor_tensor(term[:], y[:].indirect(offsets), gates[:, r * T + t0 : r * T + t1], MULT)
+            return term
+
+        head_terms = [gated(r, 0, TURNED) for r in range(TOP)]
+        tail_terms = [gated(r, TURNED, T) for r in range(TOP)]
+
+        chunks = range(TURNED // P)
+        flipped = [psum.tile([P, P], F32, name="flipped%d" % c, tag="bank%d" % c) for c in chunks]
         for r in range(TOP):
-            nc.vector.tensor_tensor(terms[r][:], y[:].indirect(token_slot[r][:]), gates[:, r * T : (r + 1) * T], MULT)
-        for t0, t1 in spans(TOKEN_CUT):
-            nc.vector.tensor_tensor(partial[:, t0:t1], terms[0][:, t0:t1], terms[1][:, t0:t1], ADD)
+            for c in chunks:
+                nc.tensor.matmul(
+                    flipped[c][:],
+                    head_terms[r][:, c * P : (c + 1) * P],
+                    identity[:],
+                    start=(r == 0),
+                    stop=(r == TOP - 1),
+                    is_transpose=True,
+                )
+        head = keep.tile([P, TURNED], F32, name="head", align_bytes=ALIGN)
+        for c in chunks:
+            flipped_sb = keep.tile([P, P], F32, name="flipped_sb%d" % c, align_bytes=ALIGN)
+            nc.scalar.copy(flipped_sb[:], flipped[c][:])
+            back = psum.tile([P, P], F32, name="back%d" % c, tag="bank%d" % (len(chunks) + c))
+            nc.tensor.transpose(back[:], flipped_sb[:], identity[:])
+            nc.scalar.copy(head[:, c * P : (c + 1) * P], back[:])
+        nc.scalar.dma_start(out[:, :TURNED], head[:])
+
+        partial = keep.tile([P, T - TURNED], F32, name="partial", align_bytes=ALIGN)
+        tail = keep.tile([P, T - TURNED], F32, name="tail", align_bytes=ALIGN)
+        nc.vector.tensor_tensor(partial[:], tail_terms[0][:], tail_terms[1][:], ADD)
         for t0, t1 in spans(STORE_CUT):
-            nc.vector.tensor_tensor(result[:, t0:t1], partial[:, t0:t1], terms[2][:, t0:t1], ADD)
-            nc.sync.dma_start(out[:, t0:t1], result[:, t0:t1])
+            cols = slice(t0 - TURNED, t1 - TURNED)
+            nc.vector.tensor_tensor(tail[:, cols], partial[:, cols], tail_terms[2][:, cols], ADD)
+            nc.sync.dma_start(out[:, t0:t1], tail[:, cols])

@@ -37,7 +37,7 @@ BANK = 512
 ALIGN = 256
 FILLER = CLOSE_CUT[1] * C
 FILLER_CUT = (0, 256, FILLER)
-STAGE_BUFS = 8
+STAGE_BUFS = 7
 LOAD_CUT = ((0, 256, 512, 640), (0, 256, 512, 640), (0, 384, 640), (0, 384, 640))
 QUANT_CUT = ((0, 256, 512, 640), (0, 512, 640), (0, 512, 640), (0, 512, 640))
 SCALE_CUT = (0, 7, 15)
@@ -45,7 +45,7 @@ SCALE_WINDOW = 1408
 SUM_ORDER = (3, 0, 1, 2)
 TURNED = 384
 STORE_CUT = (TURNED, 512, 640)
-VECTOR_SHARE = (256, 256, 128)
+VECTOR_SHARE = (256, 168, 80)
 
 
 def spans(cut):
@@ -179,14 +179,12 @@ def tile_moe_tk_lin_none_kernel(
                 for a in range(a0, a1):
                     weights[e, a] = tile[:, e - e0, a - a0, :].bitcast(dtype)
 
-        load_weights(0, 3, 0, 2)
-        load_weights(0, 3, 2, 4)
+        load_weights(0, 7, 0, 2)
         scale_words = w_scales[:].bitcast(I32)
         for row in (W8_ROW, 0):
             for r in range(1, 4):
                 nc.sync.dma_start(scale_words[row + r : P : 32, :], scale_words[row + 8 * r : P : 32, :])
-        load_weights(3, 7, 0, 2)
-        load_weights(3, 7, 2, 4)
+        load_weights(0, 7, 2, 4)
 
         for a, cut in enumerate((EARLY_CUT, EARLY_CUT, FILLER_CUT)):
             for s0, s1 in spans(cut)[:-1]:
@@ -264,7 +262,13 @@ def tile_moe_tk_lin_none_kernel(
             return term
 
         head_terms = [gated(r, 0, TURNED) for r in range(TOP)]
-        tail_terms = [gated(r, TURNED, T) for r in range(TOP)]
+        tail_terms = [gated(r, TURNED, T) for r in range(TOP - 1)]
+        partial = keep.tile([P, T - TURNED], F32, name="partial", align_bytes=ALIGN)
+        last_terms = []
+        for t0, t1 in spans(STORE_CUT):
+            last_terms.append(gated(TOP - 1, t0, t1))
+            if t0 == TURNED:
+                nc.vector.tensor_tensor(partial[:], tail_terms[0][:], tail_terms[1][:], ADD)
 
         chunks = range(TURNED // P)
         flipped = [psum.tile([P, P], F32, name="flipped%d" % c, tag="bank%d" % c) for c in chunks]
@@ -285,12 +289,10 @@ def tile_moe_tk_lin_none_kernel(
             back = psum.tile([P, P], F32, name="back%d" % c, tag="bank%d" % (len(chunks) + c))
             nc.tensor.transpose(back[:], flipped_sb[:], identity[:])
             nc.scalar.copy(head[:, c * P : (c + 1) * P], back[:])
-        nc.scalar.dma_start(out[:, :TURNED], head[:])
+            nc.sync.dma_start(out[:, c * P : (c + 1) * P], head[:, c * P : (c + 1) * P])
 
-        partial = keep.tile([P, T - TURNED], F32, name="partial", align_bytes=ALIGN)
         tail = keep.tile([P, T - TURNED], F32, name="tail", align_bytes=ALIGN)
-        nc.vector.tensor_tensor(partial[:], tail_terms[0][:], tail_terms[1][:], ADD)
-        for t0, t1 in spans(STORE_CUT):
+        for term, (t0, t1) in zip(last_terms, spans(STORE_CUT)):
             cols = slice(t0 - TURNED, t1 - TURNED)
-            nc.vector.tensor_tensor(tail[:, cols], partial[:, cols], tail_terms[2][:, cols], ADD)
+            nc.vector.tensor_tensor(tail[:, cols], partial[:, cols], term[:], ADD)
             nc.sync.dma_start(out[:, t0:t1], tail[:, cols])

@@ -43,7 +43,7 @@ QUANT_CUT = ((0, 256, 512, 640), (0, 512, 640), (0, 512, 640), (0, 512, 640))
 SCALE_CUT = (0, 7, 15)
 SCALE_WINDOW = 1408
 SUM_ORDER = (3, 0, 1, 2)
-TURNED = 384
+TURNED = 256
 STORE_CUT = (TURNED, 512, 640)
 VECTOR_SHARE = (256, 168, 80)
 
@@ -207,7 +207,8 @@ def tile_moe_tk_lin_none_kernel(
         load_weights(7, 15, 3, 4)
         gather_scales(1)
         load_weights(11, 15, 0, 2)
-        load_weights(7, 15, 2, 3)
+        load_weights(7, 11, 2, 3)
+        load_weights(11, 15, 2, 3)
         sums = {}
 
         def multiply(e, passes):

@@ -37,12 +37,11 @@ BANK = 512
 ALIGN = 256
 FILLER = CLOSE_CUT[1] * C
 FILLER_CUT = (0, 256, FILLER)
-STAGE_BUFS = 7
+STAGE_BUFS = 8
 LOAD_CUT = ((0, 256, 512, 640), (0, 256, 512, 640), (0, 384, 640), (0, 384, 640))
 QUANT_CUT = ((0, 256, 512, 640), (0, 512, 640), (0, 512, 640), (0, 512, 640))
 SCALE_CUT = (0, 7, 15)
 SCALE_WINDOW = 1408
-SUM_ORDER = (3, 0, 1, 2)
 TURNED = 256
 STORE_CUT = (TURNED, 512, 640)
 VECTOR_SHARE = (256, 168, 80)
@@ -184,7 +183,8 @@ def tile_moe_tk_lin_none_kernel(
         for row in (W8_ROW, 0):
             for r in range(1, 4):
                 nc.sync.dma_start(scale_words[row + r : P : 32, :], scale_words[row + 8 * r : P : 32, :])
-        load_weights(0, 7, 2, 4)
+        load_weights(0, 3, 2, 4)
+        load_weights(3, 7, 3, 4)
 
         for a, cut in enumerate((EARLY_CUT, EARLY_CUT, FILLER_CUT)):
             for s0, s1 in spans(cut)[:-1]:
@@ -206,9 +206,9 @@ def tile_moe_tk_lin_none_kernel(
         load_weights(7, 11, 0, 2)
         load_weights(7, 15, 3, 4)
         gather_scales(1)
+        load_weights(3, 7, 2, 3)
         load_weights(11, 15, 0, 2)
-        load_weights(7, 11, 2, 3)
-        load_weights(11, 15, 2, 3)
+        load_weights(7, 15, 2, 3)
         sums = {}
 
         def multiply(e, passes):
@@ -227,33 +227,38 @@ def tile_moe_tk_lin_none_kernel(
                     lhsT_scale=w_scales[w_row:P, m * N : (m + 1) * N],
                     rhs=slot_words[a, e],
                     rhs_scale=x_plane,
-                    start=(a == SUM_ORDER[0]),
-                    stop=(a == SUM_ORDER[-1]),
+                    start=(a == 0),
+                    stop=(a == (PASSES - 1 if e < CLOSE_CUT[1] else HALF)),
                 )
 
         def open_sums(e0, e1):
-            for e in range(e0, e1):
+            for e in range(e0, min(e1, E)):
                 sums[e] = psum.tile([P, C], F32, name="sums%d" % e, tag="bank%d" % (e % BANKS))
-                multiply(e, SUM_ORDER[:-1])
+                multiply(e, range(HALF + 1 if e < CLOSE_CUT[1] else HALF))
+
+        def third(e0, e1):
+            gather_words(PASSES - 1, e0 * C, e1 * C)
+            for e in range(e0, e1):
+                multiply(e, (PASSES - 1,))
 
         def close_sums(e0, e1):
+            if e0 > 0:
+                gather_words(HALF, e0 * C, e1 * C)
             for e in range(e0, e1):
-                multiply(e, SUM_ORDER[-1:])
+                if e0 > 0:
+                    multiply(e, (HALF,))
                 nc.scalar.copy(y[:, e * C : (e + 1) * C], sums[e][:])
+            open_sums(e0 + BANKS, e1 + BANKS)
 
         opens, closes = spans(OPEN_CUT), spans(CLOSE_CUT)
-        gather_words(PASSES - 1, opens[0][0] * C, opens[0][1] * C)
-        open_sums(*opens[0])
+        open_sums(0, BANKS)
+        third(*opens[0])
         close_sums(*closes[0])
-        gather_words(PASSES - 1, opens[1][0] * C, opens[1][1] * C)
-        open_sums(*opens[1])
-        for (o0, o1), (c0, c1) in zip(opens[2:], closes[1:]):
-            gather_words(PASSES - 1, o0 * C, o1 * C)
-            open_sums(o0, o1)
-            gather_words(HALF, c0 * C, c1 * C)
-            close_sums(c0, c1)
-        for c0, c1 in closes[len(opens) - 1 :]:
-            gather_words(HALF, c0 * C, c1 * C)
+        third(*opens[1])
+        third(*opens[2])
+        close_sums(*closes[1])
+        third(*opens[3])
+        for c0, c1 in closes[2:]:
             close_sums(c0, c1)
 
         def gated(r, t0, t1):
@@ -290,7 +295,7 @@ def tile_moe_tk_lin_none_kernel(
             back = psum.tile([P, P], F32, name="back%d" % c, tag="bank%d" % (len(chunks) + c))
             nc.tensor.transpose(back[:], flipped_sb[:], identity[:])
             nc.scalar.copy(head[:, c * P : (c + 1) * P], back[:])
-            nc.sync.dma_start(out[:, c * P : (c + 1) * P], head[:, c * P : (c + 1) * P])
+        nc.sync.dma_start(out[:, :TURNED], head[:])
 
         tail = keep.tile([P, T - TURNED], F32, name="tail", align_bytes=ALIGN)
         for term, (t0, t1) in zip(last_terms, spans(STORE_CUT)):

@@ -28,12 +28,13 @@ LIST_ROWS = 16
 PLANE_ROW = (4, 12, 0, 8)
 W8_ROW = 4
 WORD_PLACE = (3, 2, 0, 1)
-EARLY_CUT = (0, 896, 1792, 1920)
-OPEN_CUT = (0, 3, 7, 11, 15)
+EARLY_CUT = ((0, 896, 1792, 1920), (0, 1536, 1920))
+OPEN_CUT = (0, 3, 11, 15)
 CLOSE_CUT = (0, 3, 7, 11, 13, 14, 15)
 BANKS = 8
 CHUNKS = T // P
 BANK = 512
+SPARE = 768
 ALIGN = 256
 FILLER = CLOSE_CUT[1] * C
 FILLER_CUT = (0, 256, FILLER)
@@ -42,8 +43,7 @@ LOAD_CUT = ((0, 256, 512, 640), (0, 256, 512, 640), (0, 384, 640), (0, 384, 640)
 QUANT_CUT = ((0, 256, 512, 640), (0, 512, 640), (0, 512, 640), (0, 512, 640))
 SCALE_CUT = (0, 7, 15)
 SCALE_WINDOW = 1408
-TURNED = 256
-STORE_CUT = (TURNED, 512, 640)
+TURNED = 384
 VECTOR_SHARE = (256, 168, 80)
 
 
@@ -76,7 +76,7 @@ def tile_moe_tk_lin_none_kernel(
             for a in range(PASSES)
         ]
         x_bf = [keep.tile([P, T, PACK], BF16, name="x_bf%d" % a, align_bytes=ALIGN) for a in range(PASSES)]
-        tok_words = keep.tile([P, (PASSES + 1) * T], I32, name="tok_words", align_bytes=ALIGN)
+        tok_words = keep.tile([P, PASSES * T + SPARE], I32, name="tok_words", align_bytes=ALIGN)
         tok_scales = keep.tile([P, SCALE_WINDOW], U8, name="tok_scales", align_bytes=ALIGN)
         slot_words = {}
         slot_scales = [
@@ -132,7 +132,7 @@ def tile_moe_tk_lin_none_kernel(
 
         def gather_words(a, s0, s1, held=False):
             first = WORD_PLACE[a] * T
-            width = T if a == HALF and s1 <= FILLER else min(2 * T, 8 * (s1 - s0))
+            width = T if a == HALF and s1 <= FILLER else min(max(2 * T, 3 * (s1 - s0) // 2 if s1 - s0 < 1536 else 2048), 8 * (s1 - s0))
             name = "slot_words%d_%d" % (a, s0)
             words = keep.tile([P, s1 - s0], U32, name=name, tag="hold%d" % (a + 1) if held else name, align_bytes=ALIGN)
             gather(words[:], tok_words[:, first : first + width].bitcast(U32), s0, s1)
@@ -186,7 +186,7 @@ def tile_moe_tk_lin_none_kernel(
         load_weights(0, 3, 2, 4)
         load_weights(3, 7, 3, 4)
 
-        for a, cut in enumerate((EARLY_CUT, EARLY_CUT, FILLER_CUT)):
+        for a, cut in enumerate(EARLY_CUT + (FILLER_CUT,)):
             for s0, s1 in spans(cut)[:-1]:
                 gather_words(a, s0, s1)
             for piece in range(2):
@@ -204,11 +204,11 @@ def tile_moe_tk_lin_none_kernel(
 
         gather_scales(0)
         load_weights(7, 11, 0, 2)
-        load_weights(7, 15, 3, 4)
+        load_weights(7, 11, 3, 4)
         gather_scales(1)
-        load_weights(3, 7, 2, 3)
+        load_weights(3, 11, 2, 3)
         load_weights(11, 15, 0, 2)
-        load_weights(7, 15, 2, 3)
+        load_weights(11, 15, 2, 4)
         sums = {}
 
         def multiply(e, passes):
@@ -255,10 +255,10 @@ def tile_moe_tk_lin_none_kernel(
         third(*opens[0])
         close_sums(*closes[0])
         third(*opens[1])
-        third(*opens[2])
         close_sums(*closes[1])
-        third(*opens[3])
-        for c0, c1 in closes[2:]:
+        close_sums(*closes[2])
+        third(*opens[2])
+        for c0, c1 in closes[3:]:
             close_sums(c0, c1)
 
         def gated(r, t0, t1):
@@ -268,13 +268,7 @@ def tile_moe_tk_lin_none_kernel(
             return term
 
         head_terms = [gated(r, 0, TURNED) for r in range(TOP)]
-        tail_terms = [gated(r, TURNED, T) for r in range(TOP - 1)]
-        partial = keep.tile([P, T - TURNED], F32, name="partial", align_bytes=ALIGN)
-        last_terms = []
-        for t0, t1 in spans(STORE_CUT):
-            last_terms.append(gated(TOP - 1, t0, t1))
-            if t0 == TURNED:
-                nc.vector.tensor_tensor(partial[:], tail_terms[0][:], tail_terms[1][:], ADD)
+        tail_terms = [gated(r, TURNED, T) for r in range(TOP)]
 
         chunks = range(TURNED // P)
         flipped = [psum.tile([P, P], F32, name="flipped%d" % c, tag="bank%d" % c) for c in chunks]
@@ -295,10 +289,12 @@ def tile_moe_tk_lin_none_kernel(
             back = psum.tile([P, P], F32, name="back%d" % c, tag="bank%d" % (len(chunks) + c))
             nc.tensor.transpose(back[:], flipped_sb[:], identity[:])
             nc.scalar.copy(head[:, c * P : (c + 1) * P], back[:])
-        nc.sync.dma_start(out[:, :TURNED], head[:])
+            if c > 0:
+                t0 = 0 if c == 1 else c * P
+                nc.sync.dma_start(out[:, t0 : (c + 1) * P], head[:, t0 : (c + 1) * P])
 
+        partial = keep.tile([P, T - TURNED], F32, name="partial", align_bytes=ALIGN)
         tail = keep.tile([P, T - TURNED], F32, name="tail", align_bytes=ALIGN)
-        for term, (t0, t1) in zip(last_terms, spans(STORE_CUT)):
-            cols = slice(t0 - TURNED, t1 - TURNED)
-            nc.vector.tensor_tensor(tail[:, cols], partial[:, cols], term[:], ADD)
-            nc.sync.dma_start(out[:, t0:t1], tail[:, cols])
+        nc.vector.tensor_tensor(partial[:], tail_terms[0][:], tail_terms[1][:], ADD)
+        nc.vector.tensor_tensor(tail[:], partial[:], tail_terms[2][:], ADD)
+        nc.sync.dma_start(out[:, TURNED:], tail[:])

@@ -18,6 +18,7 @@ FP8X4 = mybir.dt.float8_e4m3fn_x4
 FP4X4 = mybir.dt.float4_e2m1fn_x4
 MULT = mybir.AluOpType.mult
 ADD = mybir.AluOpType.add
+COPY = mybir.ActivationFunctionType.Copy
 
 P = 128
 PACK = 4
@@ -28,27 +29,31 @@ LIST_ROWS = 16
 PLANE_ROW = (4, 12, 0, 8)
 W8_ROW = 4
 WORD_PLACE = (3, 2, 0, 1)
-EARLY_CUT = ((0, 896, 1792, 1920), (0, 1536, 1920))
-OPEN_CUT = (0, 3, 11, 15)
-CLOSE_CUT = (0, 3, 7, 11, 13, 14, 15)
+EARLY = 1792
+FIRST = 3
+THIRD_CUT = (0, FIRST, 11, E)
+CLOSE_CUT = (FIRST, 7, 11, 13, 14, E)
 BANKS = 8
 CHUNKS = T // P
-BANK = 512
-SPARE = 768
+SPARE = 2 * EARLY - T
 ALIGN = 256
-FILLER = CLOSE_CUT[1] * C
-FILLER_CUT = (0, 256, FILLER)
 STAGE_BUFS = 8
 LOAD_CUT = ((0, 256, 512, 640), (0, 256, 512, 640), (0, 384, 640), (0, 384, 640))
 QUANT_CUT = ((0, 256, 512, 640), (0, 512, 640), (0, 512, 640), (0, 512, 640))
-SCALE_CUT = (0, 7, 15)
+SCALE_CUT = (0, 7, E)
 SCALE_WINDOW = 1408
-TURNED = 384
+TURNED = 3
 VECTOR_SHARE = (256, 168, 80)
 
 
 def spans(cut):
     return list(zip(cut[:-1], cut[1:]))
+
+
+def window_width(entries):
+    if entries > 1536:
+        return 2 * entries
+    return max(T, min(3 * entries // 2, 2048))
 
 
 def tile_moe_tk_lin_none_kernel(
@@ -61,42 +66,42 @@ def tile_moe_tk_lin_none_kernel(
         stage = ctx.enter_context(tc.tile_pool(name="stage", bufs=STAGE_BUFS))
         psum = ctx.enter_context(tc.psum_pool(name="psum", bufs=1))
 
+        def kept(shape, dtype, name, tag=None):
+            return keep.tile(shape, dtype, name=name, tag=tag or name, align_bytes=ALIGN)
+
+        def bank(width, name, b):
+            return psum.tile([P, width], F32, name=name, tag="bank%d" % b)
+
         slot_token = lists.tile([P, S // LIST_ROWS], U16, name="slot_token")
         token_slot = [lists.tile([P, T // LIST_ROWS], U16, name="token_slot%d" % r) for r in range(TOP)]
 
-        x_raw = [
-            [
-                keep.tile([P, PACK, t1 - t0], F32, name="x_last%d" % a, tag="hold%d" % a, align_bytes=ALIGN)
-                if a > 0 and t1 == T
-                else keep.tile([P, PACK, t1 - t0], F32, name="x_late", tag="gates", align_bytes=ALIGN)
-                if a == PASSES - 1
-                else stage.tile([P, PACK, t1 - t0], F32, name="x_raw%d_%d" % (a, t0), tag="stage", align_bytes=ALIGN)
-                for t0, t1 in spans(LOAD_CUT[a])
-            ]
-            for a in range(PASSES)
-        ]
-        x_bf = [keep.tile([P, T, PACK], BF16, name="x_bf%d" % a, align_bytes=ALIGN) for a in range(PASSES)]
-        tok_words = keep.tile([P, PASSES * T + SPARE], I32, name="tok_words", align_bytes=ALIGN)
-        tok_scales = keep.tile([P, SCALE_WINDOW], U8, name="tok_scales", align_bytes=ALIGN)
-        slot_words = {}
-        slot_scales = [
-            keep.tile([P, (e1 - e0) * C], U8, name="slot_scales%d" % e0, align_bytes=ALIGN) for e0, e1 in spans(SCALE_CUT)
-        ]
-        last_scales = [
-            keep.tile([P, (e1 - e0) * C], U8, name="last_scales%d" % e0, align_bytes=ALIGN) for e0, e1 in spans(SCALE_CUT)
-        ]
-        w_scales = keep.tile([P, E * HALF * N], U8, name="w_scales", align_bytes=ALIGN)
-        y = keep.tile([P, S], F32, name="y", align_bytes=ALIGN)
+        def raw_tile(a, t0, t1):
+            shape = [P, PACK, t1 - t0]
+            if a > 0 and t1 == T:
+                return kept(shape, F32, "x_last%d" % a, "hold%d" % a)
+            if a == PASSES - 1:
+                return kept(shape, F32, "x_late", "late")
+            return stage.tile(shape, F32, name="x_raw%d_%d" % (a, t0), tag="stage", align_bytes=ALIGN)
 
-        identity = keep.tile([P, P], F32, name="identity", align_bytes=ALIGN)
-        gate_rows = keep.tile([P, P], F32, name="gate_rows", align_bytes=ALIGN)
-        gate_cols = keep.tile([P, TOP * CHUNKS], F32, name="gate_cols", align_bytes=ALIGN)
+        x_raw = [[raw_tile(a, t0, t1) for t0, t1 in spans(LOAD_CUT[a])] for a in range(PASSES)]
+        x_bf = [kept([P, T, PACK], BF16, "x_bf%d" % a) for a in range(PASSES)]
+        tok_words = kept([P, PASSES * T + SPARE], I32, "tok_words")
+        tok_scales = kept([P, SCALE_WINDOW], U8, "tok_scales")
+        slot_words = {}
+        slot_scales = [kept([P, (e1 - e0) * C], U8, "slot_scales%d" % e0) for e0, e1 in spans(SCALE_CUT)]
+        last_scales = [kept([P, (e1 - e0) * C], U8, "last_scales%d" % e0) for e0, e1 in spans(SCALE_CUT)]
+        w_scales = kept([P, E * HALF * N], U8, "w_scales")
+        y = kept([P, S], F32, "y")
+        identity = kept([P, P], F32, "identity")
+        gate_rows = kept([P, P], F32, "gate_rows")
+        gate_cols = kept([P, TOP * CHUNKS], F32, "gate_cols")
+
         make_identity(nc, identity[:])
         nc.vector.memset(gate_rows[:], 0.0)
         nc.scalar.dma_start(gate_rows[: TOP * CHUNKS, :], gate.rearrange("r n (c t) -> (r n c) t", t=P)[::P, :])
-        for plane in [w_scales, tok_scales] + last_scales:
+        for plane in [w_scales] + last_scales:
             nc.vector.memset(plane[:].bitcast(I32), 0)
-        nc.vector.memset(tok_words[:, PASSES * T :], 0)
+        nc.vector.memset(tok_scales[:, :T].bitcast(I32), 0)
 
         for a in range(PASSES):
             rows = xT[a * K_PASS : (a + 1) * K_PASS, :].rearrange("(p j) t -> p j t", j=PACK)
@@ -127,14 +132,14 @@ def tile_moe_tk_lin_none_kernel(
             )
 
         def gather(dst, window, s0, s1):
-            offsets = slot_token[:, s0 // LIST_ROWS : s1 // LIST_ROWS]
-            nc.vector.tensor_copy(dst, window.indirect(offsets))
+            nc.vector.tensor_copy(dst, window.indirect(slot_token[:, s0 // LIST_ROWS : s1 // LIST_ROWS]))
 
-        def gather_words(a, s0, s1, held=False):
+        def gather_words(a, s0, s1, tag=None):
             first = WORD_PLACE[a] * T
-            width = T if a == HALF and s1 <= FILLER else min(max(2 * T, 3 * (s1 - s0) // 2 if s1 - s0 < 1536 else 2048), 8 * (s1 - s0))
-            name = "slot_words%d_%d" % (a, s0)
-            words = keep.tile([P, s1 - s0], U32, name=name, tag="hold%d" % (a + 1) if held else name, align_bytes=ALIGN)
+            width = window_width(s1 - s0)
+            if a == HALF and tag is None:
+                width = max(width, min(2 * T, 8 * (s1 - s0)))
+            words = kept([P, s1 - s0], U32, "slot_words%d_%d" % (a, s0), tag)
             gather(words[:], tok_words[:, first : first + width].bitcast(U32), s0, s1)
             for s in range(s0, s1, C):
                 slot_words[a, s // C] = words[:, s - s0 : s - s0 + C].bitcast(FP8X4)
@@ -149,20 +154,21 @@ def tile_moe_tk_lin_none_kernel(
             for piece in range(len(x_raw[a])):
                 round_tokens(a, piece)
 
-        turned = psum.tile([P, P], F32, name="turned", tag="bank3")
-        nc.tensor.transpose(turned[:], gate_rows[:], identity[:])
-        nc.scalar.copy(gate_cols[:], turned[:, : TOP * CHUNKS])
-        gates = keep.tile([P, TOP * T], F32, name="gates", tag="gates", align_bytes=ALIGN)
-        for b, t0 in enumerate(range(0, TOP * T, BANK)):
-            t1 = min(t0 + BANK, TOP * T)
-            spread = psum.tile([P, t1 - t0], F32, name="spread%d" % b, tag="bank%d" % (4 + b))
-            for t in range(t0, t1, P):
-                r, c = divmod(t // P, CHUNKS)
-                col = r * CHUNKS + 2 * c % CHUNKS
-                nc.tensor.transpose(
-                    spread[:, t - t0 : t - t0 + P], gate_cols[:, col : col + 1].to_broadcast([P, P]), identity[:]
-                )
-            nc.scalar.copy(gates[:, t0:t1], spread[:])
+        def gate_col(r, c):
+            col = r * CHUNKS + 2 * c % CHUNKS
+            return gate_cols[:, col : col + 1]
+
+        turned_gate = bank(P, "turned_gate", 3)
+        nc.tensor.transpose(turned_gate[:], gate_rows[:], identity[:])
+        nc.scalar.copy(gate_cols[:], turned_gate[:, : TOP * CHUNKS])
+        rest = T - TURNED * P
+        gates = kept([P, TOP, rest], F32, "gates", "late")
+        for r in range(TOP):
+            spread = bank(rest, "spread%d" % r, 4 + r)
+            for c in range(TURNED, CHUNKS):
+                t0 = (c - TURNED) * P
+                nc.tensor.transpose(spread[:, t0 : t0 + P], gate_col(r, c).to_broadcast([P, P]), identity[:])
+            nc.scalar.copy(gates[:, r, :], spread[:])
 
         w8_src = w8_words.rearrange("e a p n t -> p e a (n t)").bitcast(I32)
         w4_src = w4_words.rearrange("e a p b -> p e a b").bitcast(I32)
@@ -186,12 +192,14 @@ def tile_moe_tk_lin_none_kernel(
         load_weights(0, 3, 2, 4)
         load_weights(3, 7, 3, 4)
 
-        for a, cut in enumerate(EARLY_CUT + (FILLER_CUT,)):
-            for s0, s1 in spans(cut)[:-1]:
-                gather_words(a, s0, s1)
+        for a in range(HALF):
+            gather_words(a, 0, EARLY)
             for piece in range(2):
                 quantize_tokens(a + 1, piece)
-            gather_words(a, cut[-2], cut[-1], held=True)
+            gather_words(a, EARLY, S, "hold%d" % (a + 1))
+        for piece in range(2):
+            quantize_tokens(PASSES - 1, piece)
+        gather_words(HALF, 0, FIRST * C, "hold%d" % (PASSES - 1))
 
         def gather_scales(half):
             e0, e1 = spans(SCALE_CUT)[half]
@@ -228,73 +236,73 @@ def tile_moe_tk_lin_none_kernel(
                     rhs=slot_words[a, e],
                     rhs_scale=x_plane,
                     start=(a == 0),
-                    stop=(a == (PASSES - 1 if e < CLOSE_CUT[1] else HALF)),
+                    stop=(a == (PASSES - 1 if e < FIRST else HALF)),
                 )
 
         def open_sums(e0, e1):
             for e in range(e0, min(e1, E)):
-                sums[e] = psum.tile([P, C], F32, name="sums%d" % e, tag="bank%d" % (e % BANKS))
-                multiply(e, range(HALF + 1 if e < CLOSE_CUT[1] else HALF))
+                sums[e] = bank(C, "sums%d" % e, e % BANKS)
+                multiply(e, range(HALF + 1 if e < FIRST else HALF))
 
         def third(e0, e1):
             gather_words(PASSES - 1, e0 * C, e1 * C)
             for e in range(e0, e1):
                 multiply(e, (PASSES - 1,))
 
-        def close_sums(e0, e1):
-            if e0 > 0:
-                gather_words(HALF, e0 * C, e1 * C)
+        def empty(e0, e1):
             for e in range(e0, e1):
-                if e0 > 0:
-                    multiply(e, (HALF,))
                 nc.scalar.copy(y[:, e * C : (e + 1) * C], sums[e][:])
             open_sums(e0 + BANKS, e1 + BANKS)
 
-        opens, closes = spans(OPEN_CUT), spans(CLOSE_CUT)
+        def close_sums(e0, e1):
+            gather_words(HALF, e0 * C, e1 * C)
+            for e in range(e0, e1):
+                multiply(e, (HALF,))
+            empty(e0, e1)
+
+        thirds, closes = spans(THIRD_CUT), spans(CLOSE_CUT)
         open_sums(0, BANKS)
-        third(*opens[0])
+        third(*thirds[0])
+        empty(*thirds[0])
+        third(*thirds[1])
         close_sums(*closes[0])
-        third(*opens[1])
         close_sums(*closes[1])
-        close_sums(*closes[2])
-        third(*opens[2])
-        for c0, c1 in closes[3:]:
+        third(*thirds[2])
+        for c0, c1 in closes[2:]:
             close_sums(c0, c1)
 
-        def gated(r, t0, t1):
-            term = keep.tile([P, t1 - t0], F32, name="term%d_%d" % (r, t0), align_bytes=ALIGN)
-            offsets = token_slot[r][:, t0 // LIST_ROWS : t1 // LIST_ROWS]
-            nc.vector.tensor_tensor(term[:], y[:].indirect(offsets), gates[:, r * T + t0 : r * T + t1], MULT)
-            return term
-
-        head_terms = [gated(r, 0, TURNED) for r in range(TOP)]
-        tail_terms = [gated(r, TURNED, T) for r in range(TOP)]
-
-        chunks = range(TURNED // P)
-        flipped = [psum.tile([P, P], F32, name="flipped%d" % c, tag="bank%d" % c) for c in chunks]
+        head_width = TURNED * P
+        back = [bank(P, "back%d" % c, c) for c in range(TURNED)]
         for r in range(TOP):
-            for c in chunks:
-                nc.tensor.matmul(
-                    flipped[c][:],
-                    head_terms[r][:, c * P : (c + 1) * P],
-                    identity[:],
-                    start=(r == 0),
-                    stop=(r == TOP - 1),
-                    is_transpose=True,
-                )
-        head = keep.tile([P, TURNED], F32, name="head", align_bytes=ALIGN)
-        for c in chunks:
-            flipped_sb = keep.tile([P, P], F32, name="flipped_sb%d" % c, align_bytes=ALIGN)
-            nc.scalar.copy(flipped_sb[:], flipped[c][:])
-            back = psum.tile([P, P], F32, name="back%d" % c, tag="bank%d" % (len(chunks) + c))
-            nc.tensor.transpose(back[:], flipped_sb[:], identity[:])
-            nc.scalar.copy(head[:, c * P : (c + 1) * P], back[:])
+            picked = kept([P, head_width], F32, "picked%d" % r)
+            nc.vector.tensor_copy(picked[:], y[:].indirect(token_slot[r][:, : head_width // LIST_ROWS]))
+            groups = [range(c, c + 1) for c in range(TURNED)]
+            for g, chunks in enumerate(groups):
+                turned = bank(len(chunks) * P, "turned%d_%d" % (r, g), TURNED + g)
+                for i, c in enumerate(chunks):
+                    nc.tensor.transpose(turned[:, i * P : (i + 1) * P], picked[:, c * P : (c + 1) * P], identity[:])
+                for i, c in enumerate(chunks):
+                    scaled = kept([P, P], F32, "scaled%d_%d" % (r, c))
+                    nc.scalar.activation(scaled[:], turned[:, i * P : (i + 1) * P], COPY, scale=gate_col(r, c))
+                    nc.tensor.matmul(
+                        back[c][:], scaled[:], identity[:], start=(r == 0), stop=(r == TOP - 1), is_transpose=True
+                    )
+        terms = []
+        for r in range(TOP):
+            term = kept([P, rest], F32, "term%d" % r)
+            offsets = token_slot[r][:, head_width // LIST_ROWS :]
+            nc.vector.tensor_tensor(term[:], y[:].indirect(offsets), gates[:, r, :], MULT)
+            terms.append(term)
+
+        head = kept([P, head_width], F32, "head")
+        for c in range(TURNED):
+            nc.scalar.copy(head[:, c * P : (c + 1) * P], back[c][:])
             if c > 0:
                 t0 = 0 if c == 1 else c * P
                 nc.sync.dma_start(out[:, t0 : (c + 1) * P], head[:, t0 : (c + 1) * P])
 
-        partial = keep.tile([P, T - TURNED], F32, name="partial", align_bytes=ALIGN)
-        tail = keep.tile([P, T - TURNED], F32, name="tail", align_bytes=ALIGN)
-        nc.vector.tensor_tensor(partial[:], tail_terms[0][:], tail_terms[1][:], ADD)
-        nc.vector.tensor_tensor(tail[:], partial[:], tail_terms[2][:], ADD)
-        nc.sync.dma_start(out[:, TURNED:], tail[:])
+        partial = kept([P, rest], F32, "partial")
+        tail = kept([P, rest], F32, "tail")
+        nc.vector.tensor_tensor(partial[:], terms[0][:], terms[1][:], ADD)
+        nc.vector.tensor_tensor(tail[:], partial[:], terms[2][:], ADD)
+        nc.sync.dma_start(out[:, head_width:], tail[:])

@@ -18,7 +18,6 @@ FP8X4 = mybir.dt.float8_e4m3fn_x4
 FP4X4 = mybir.dt.float4_e2m1fn_x4
 MULT = mybir.AluOpType.mult
 ADD = mybir.AluOpType.add
-COPY = mybir.ActivationFunctionType.Copy
 
 P = 128
 PACK = 4
@@ -34,6 +33,7 @@ FIRST = 3
 THIRD_CUT = (0, FIRST, 11, E)
 CLOSE_CUT = (FIRST, 7, 11, 13, 14, E)
 BANKS = 8
+BANK = 512
 CHUNKS = T // P
 SPARE = 2 * EARLY - T
 ALIGN = 256
@@ -162,13 +162,14 @@ def tile_moe_tk_lin_none_kernel(
         nc.tensor.transpose(turned_gate[:], gate_rows[:], identity[:])
         nc.scalar.copy(gate_cols[:], turned_gate[:, : TOP * CHUNKS])
         rest = T - TURNED * P
-        gates = kept([P, TOP, rest], F32, "gates", "late")
-        for r in range(TOP):
-            spread = bank(rest, "spread%d" % r, 4 + r)
-            for c in range(TURNED, CHUNKS):
-                t0 = (c - TURNED) * P
-                nc.tensor.transpose(spread[:, t0 : t0 + P], gate_col(r, c).to_broadcast([P, P]), identity[:])
-            nc.scalar.copy(gates[:, r, :], spread[:])
+        gates = kept([P, TOP * T], F32, "gates", "late")
+        for b, t0 in enumerate(range(0, TOP * T, BANK)):
+            t1 = min(t0 + BANK, TOP * T)
+            spread = bank(t1 - t0, "spread%d" % b, 4 + b)
+            for t in range(t0, t1, P):
+                column = gate_col(*divmod(t // P, CHUNKS))
+                nc.tensor.transpose(spread[:, t - t0 : t - t0 + P], column.to_broadcast([P, P]), identity[:])
+            nc.scalar.copy(gates[:, t0:t1], spread[:])
 
         w8_src = w8_words.rearrange("e a p n t -> p e a (n t)").bitcast(I32)
         w4_src = w4_words.rearrange("e a p b -> p e a b").bitcast(I32)
@@ -272,31 +273,33 @@ def tile_moe_tk_lin_none_kernel(
             close_sums(c0, c1)
 
         head_width = TURNED * P
-        back = [bank(P, "back%d" % c, c) for c in range(TURNED)]
-        for r in range(TOP):
-            picked = kept([P, head_width], F32, "picked%d" % r)
-            nc.vector.tensor_copy(picked[:], y[:].indirect(token_slot[r][:, : head_width // LIST_ROWS]))
-            groups = [range(c, c + 1) for c in range(TURNED)]
-            for g, chunks in enumerate(groups):
-                turned = bank(len(chunks) * P, "turned%d_%d" % (r, g), TURNED + g)
-                for i, c in enumerate(chunks):
-                    nc.tensor.transpose(turned[:, i * P : (i + 1) * P], picked[:, c * P : (c + 1) * P], identity[:])
-                for i, c in enumerate(chunks):
-                    scaled = kept([P, P], F32, "scaled%d_%d" % (r, c))
-                    nc.scalar.activation(scaled[:], turned[:, i * P : (i + 1) * P], COPY, scale=gate_col(r, c))
-                    nc.tensor.matmul(
-                        back[c][:], scaled[:], identity[:], start=(r == 0), stop=(r == TOP - 1), is_transpose=True
-                    )
-        terms = []
-        for r in range(TOP):
-            term = kept([P, rest], F32, "term%d" % r)
-            offsets = token_slot[r][:, head_width // LIST_ROWS :]
-            nc.vector.tensor_tensor(term[:], y[:].indirect(offsets), gates[:, r, :], MULT)
-            terms.append(term)
 
+        def gated(r, t0, t1):
+            term = kept([P, t1 - t0], F32, "term%d_%d" % (r, t0))
+            offsets = token_slot[r][:, t0 // LIST_ROWS : t1 // LIST_ROWS]
+            nc.vector.tensor_tensor(term[:], y[:].indirect(offsets), gates[:, r * T + t0 : r * T + t1], MULT)
+            return term
+
+        head_terms = [gated(r, 0, head_width) for r in range(TOP)]
+        terms = [gated(r, head_width, T) for r in range(TOP)]
+        flipped = [bank(P, "flipped%d" % c, c) for c in range(TURNED)]
+        for r in range(TOP):
+            for c in range(TURNED):
+                nc.tensor.matmul(
+                    flipped[c][:],
+                    head_terms[r][:, c * P : (c + 1) * P],
+                    identity[:],
+                    start=(r == 0),
+                    stop=(r == TOP - 1),
+                    is_transpose=True,
+                )
         head = kept([P, head_width], F32, "head")
         for c in range(TURNED):
-            nc.scalar.copy(head[:, c * P : (c + 1) * P], back[c][:])
+            flipped_sb = kept([P, P], F32, "flipped_sb%d" % c)
+            nc.scalar.copy(flipped_sb[:], flipped[c][:])
+            back = bank(P, "back%d" % c, TURNED + c)
+            nc.tensor.transpose(back[:], flipped_sb[:], identity[:])
+            nc.scalar.copy(head[:, c * P : (c + 1) * P], back[:])
             if c > 0:
                 t0 = 0 if c == 1 else c * P
                 nc.sync.dma_start(out[:, t0 : (c + 1) * P], head[:, t0 : (c + 1) * P])

@@ -27,7 +27,8 @@ HALF = PASSES // 2
 LIST_ROWS = 16
 PLANE_ROW = (4, 12, 0, 8)
 W8_ROW = 4
-WORD_PLACE = (3, 2, 0, 1)
+GAP = 128
+WORD_START = (3 * T + GAP, 2 * T + GAP, 0, T + GAP)
 EARLY = 1792
 FIRST = 3
 THIRD_CUT = (0, FIRST, 11, E)
@@ -41,7 +42,7 @@ STAGE_BUFS = 8
 LOAD_CUT = ((0, 256, 512, 640), (0, 256, 512, 640), (0, 384, 640), (0, 384, 640))
 QUANT_CUT = ((0, 256, 512, 640), (0, 512, 640), (0, 512, 640), (0, 512, 640))
 SCALE_CUT = (0, 7, E)
-SCALE_WINDOW = 1408
+SCALE_WINDOW = 1536
 TURNED = 3
 VECTOR_SHARE = (256, 168, 80)
 
@@ -85,7 +86,7 @@ def tile_moe_tk_lin_none_kernel(
 
         x_raw = [[raw_tile(a, t0, t1) for t0, t1 in spans(LOAD_CUT[a])] for a in range(PASSES)]
         x_bf = [kept([P, T, PACK], BF16, "x_bf%d" % a) for a in range(PASSES)]
-        tok_words = kept([P, PASSES * T + SPARE], I32, "tok_words")
+        tok_words = kept([P, PASSES * T + GAP + SPARE], I32, "tok_words")
         tok_scales = kept([P, SCALE_WINDOW], U8, "tok_scales")
         slot_words = {}
         slot_scales = [kept([P, (e1 - e0) * C], U8, "slot_scales%d" % e0) for e0, e1 in spans(SCALE_CUT)]
@@ -126,7 +127,7 @@ def tile_moe_tk_lin_none_kernel(
         def quantize_tokens(a, piece):
             t0, t1 = spans(QUANT_CUT[a])[piece]
             nc.vector.quantize_mx(
-                out=tok_words[:, WORD_PLACE[a] * T + t0 : WORD_PLACE[a] * T + t1].bitcast(FP8X4),
+                out=tok_words[:, WORD_START[a] + t0 : WORD_START[a] + t1].bitcast(FP8X4),
                 scales=tok_scales[PLANE_ROW[a] : P, t0:t1],
                 in_=x_bf[a][:, t0:t1, :].rearrange("p t j -> p (t j)"),
             )
@@ -135,10 +136,10 @@ def tile_moe_tk_lin_none_kernel(
             nc.vector.tensor_copy(dst, window.indirect(slot_token[:, s0 // LIST_ROWS : s1 // LIST_ROWS]))
 
         def gather_words(a, s0, s1, tag=None):
-            first = WORD_PLACE[a] * T
+            first = WORD_START[a]
             width = window_width(s1 - s0)
             if a == HALF and tag is None:
-                width = max(width, min(2 * T, 8 * (s1 - s0)))
+                width = max(width, 1024)
             words = kept([P, s1 - s0], U32, "slot_words%d_%d" % (a, s0), tag)
             gather(words[:], tok_words[:, first : first + width].bitcast(U32), s0, s1)
             for s in range(s0, s1, C):

@@ -31,7 +31,7 @@ GAP = 128
 WORD_START = (3 * T + GAP, 2 * T + GAP, 0, T + GAP)
 EARLY = 1792
 FIRST = 3
-THIRD_CUT = (0, FIRST, 11, E)
+THIRD_CUT = (0, FIRST, 7, E)
 CLOSE_CUT = (FIRST, 7, 11, 13, 14, E)
 BANKS = 8
 BANK = 512
@@ -186,13 +186,13 @@ def tile_moe_tk_lin_none_kernel(
                 for a in range(a0, a1):
                     weights[e, a] = tile[:, e - e0, a - a0, :].bitcast(dtype)
 
-        load_weights(0, 7, 0, 2)
+        load_weights(0, 4, 0, 2)
         scale_words = w_scales[:].bitcast(I32)
         for row in (W8_ROW, 0):
             for r in range(1, 4):
                 nc.sync.dma_start(scale_words[row + r : P : 32, :], scale_words[row + 8 * r : P : 32, :])
+        load_weights(4, 7, 0, 2)
         load_weights(0, 3, 2, 4)
-        load_weights(3, 7, 3, 4)
 
         for a in range(HALF):
             gather_words(a, 0, EARLY)
@@ -206,6 +206,8 @@ def tile_moe_tk_lin_none_kernel(
         def gather_scales(half):
             e0, e1 = spans(SCALE_CUT)[half]
             gather(slot_scales[half][:], tok_scales[:], e0 * C, e1 * C)
+
+        def move_scales(half):
             row = PLANE_ROW[PASSES - 1]
             for p0, p1 in ((0, 64), (64, 68), (96, 100)):
                 nc.sync.dma_start(
@@ -213,12 +215,14 @@ def tile_moe_tk_lin_none_kernel(
                 )
 
         gather_scales(0)
-        load_weights(7, 11, 0, 2)
-        load_weights(7, 11, 3, 4)
         gather_scales(1)
-        load_weights(3, 11, 2, 3)
+        move_scales(0)
+        load_weights(7, 11, 0, 2)
+        load_weights(3, 7, 2, 4)
         load_weights(11, 15, 0, 2)
-        load_weights(11, 15, 2, 4)
+        move_scales(1)
+        load_weights(7, 15, 3, 4)
+        load_weights(7, 15, 2, 3)
         sums = {}
 
         def multiply(e, passes):
@@ -268,9 +272,8 @@ def tile_moe_tk_lin_none_kernel(
         empty(*thirds[0])
         third(*thirds[1])
         close_sums(*closes[0])
-        close_sums(*closes[1])
         third(*thirds[2])
-        for c0, c1 in closes[2:]:
+        for c0, c1 in closes[1:]:
             close_sums(c0, c1)
 
         head_width = TURNED * P

@@ -30,9 +30,8 @@ W8_ROW = 4
 GAP = 128
 WORD_START = (3 * T + GAP, 2 * T + GAP, 0, T + GAP)
 EARLY = 1792
-FIRST = 3
-THIRD_CUT = (0, FIRST, 7, E)
-CLOSE_CUT = (FIRST, 7, 11, 13, 14, E)
+FIRST = 4
+CLOSE_CUT = (FIRST, 8, 12, 14, E)
 BANKS = 8
 BANK = 512
 CHUNKS = T // P
@@ -41,7 +40,7 @@ ALIGN = 256
 STAGE_BUFS = 8
 LOAD_CUT = ((0, 256, 512, 640), (0, 256, 512, 640), (0, 384, 640), (0, 384, 640))
 QUANT_CUT = ((0, 256, 512, 640), (0, 512, 640), (0, 512, 640), (0, 512, 640))
-SCALE_CUT = (0, 7, E)
+SCALE_CUT = (0, 8, E)
 SCALE_WINDOW = 1536
 TURNED = 3
 VECTOR_SHARE = (256, 168, 80)
@@ -191,8 +190,8 @@ def tile_moe_tk_lin_none_kernel(
         for row in (W8_ROW, 0):
             for r in range(1, 4):
                 nc.sync.dma_start(scale_words[row + r : P : 32, :], scale_words[row + 8 * r : P : 32, :])
-        load_weights(4, 7, 0, 2)
-        load_weights(0, 3, 2, 4)
+        load_weights(4, 8, 0, 2)
+        load_weights(0, 4, 2, 4)
 
         for a in range(HALF):
             gather_words(a, 0, EARLY)
@@ -217,12 +216,12 @@ def tile_moe_tk_lin_none_kernel(
         gather_scales(0)
         gather_scales(1)
         move_scales(0)
-        load_weights(7, 11, 0, 2)
-        load_weights(3, 7, 2, 4)
-        load_weights(11, 15, 0, 2)
+        load_weights(8, 12, 0, 2)
+        load_weights(4, 8, 2, 4)
+        load_weights(12, 15, 0, 2)
         move_scales(1)
-        load_weights(7, 15, 3, 4)
-        load_weights(7, 15, 2, 3)
+        load_weights(8, 15, 3, 4)
+        load_weights(8, 15, 2, 3)
         sums = {}
 
         def multiply(e, passes):
@@ -251,7 +250,6 @@ def tile_moe_tk_lin_none_kernel(
                 multiply(e, range(HALF + 1 if e < FIRST else HALF))
 
         def third(e0, e1):
-            gather_words(PASSES - 1, e0 * C, e1 * C)
             for e in range(e0, e1):
                 multiply(e, (PASSES - 1,))
 
@@ -266,13 +264,15 @@ def tile_moe_tk_lin_none_kernel(
                 multiply(e, (HALF,))
             empty(e0, e1)
 
-        thirds, closes = spans(THIRD_CUT), spans(CLOSE_CUT)
+        closes = spans(CLOSE_CUT)
         open_sums(0, BANKS)
-        third(*thirds[0])
-        empty(*thirds[0])
-        third(*thirds[1])
+        gather_words(PASSES - 1, 0, BANKS * C)
+        third(0, FIRST)
+        empty(0, FIRST)
+        third(FIRST, BANKS)
         close_sums(*closes[0])
-        third(*thirds[2])
+        gather_words(PASSES - 1, BANKS * C, S)
+        third(BANKS, E)
         for c0, c1 in closes[1:]:
             close_sums(c0, c1)
 

@@ -43,6 +43,7 @@ QUANT_CUT = ((0, 256, 512, 640), (0, 512, 640), (0, 512, 640), (0, 512, 640))
 SCALE_CUT = (0, 8, E)
 SCALE_WINDOW = 1536
 TURNED = 3
+WARM = 3
 VECTOR_SHARE = (256, 168, 80)
 
 
@@ -184,8 +185,9 @@ def tile_moe_tk_lin_none_kernel(
             for e in range(e0, e1):
                 for a in range(a0, a1):
                     weights[e, a] = tile[:, e - e0, a - a0, :].bitcast(dtype)
+            return tile
 
-        load_weights(0, 4, 0, 2)
+        first_weights = load_weights(0, 4, 0, 2)
         scale_words = w_scales[:].bitcast(I32)
         for row in (W8_ROW, 0):
             for r in range(1, 4):
@@ -255,7 +257,8 @@ def tile_moe_tk_lin_none_kernel(
 
         def empty(e0, e1):
             for e in range(e0, e1):
-                nc.scalar.copy(y[:, e * C : (e + 1) * C], sums[e][:])
+                copy = nc.vector.tensor_copy if e in (E - 3, E - 1) else nc.scalar.copy
+                copy(y[:, e * C : (e + 1) * C], sums[e][:])
             open_sums(e0 + BANKS, e1 + BANKS)
 
         def close_sums(e0, e1):
@@ -265,7 +268,20 @@ def tile_moe_tk_lin_none_kernel(
             empty(e0, e1)
 
         closes = spans(CLOSE_CUT)
-        open_sums(0, BANKS)
+        open_sums(0, BANKS - 1)
+        spare = bank(BANK, "spare", BANKS - 1)
+        wide = slice(0, BANK)
+        for repeat in range(WARM):
+            nc.tensor.matmul_mx(
+                out=spare[:],
+                lhsT=weights[0, 0],
+                lhsT_scale=w_scales[W8_ROW:P, :N],
+                rhs=first_weights[:].rearrange("p e a b -> p (e a b)")[:, : 4 * BANK].bitcast(FP8X4),
+                rhs_scale=w_scales[W8_ROW:P, wide],
+                start=True,
+                stop=True,
+            )
+        open_sums(BANKS - 1, BANKS)
         gather_words(PASSES - 1, 0, BANKS * C)
         third(0, FIRST)
         empty(0, FIRST)

@@ -43,7 +43,6 @@ QUANT_CUT = ((0, 256, 512, 640), (0, 512, 640), (0, 512, 640), (0, 512, 640))
 SCALE_CUT = (0, 8, E)
 SCALE_WINDOW = 1536
 TURNED = 3
-WARM = 3
 VECTOR_SHARE = (256, 168, 80)
 
 
@@ -110,8 +109,6 @@ def tile_moe_tk_lin_none_kernel(
                 nc.sync.dma_start(raw[:], rows[:, :, t0:t1])
             if a == 0:
                 nc.sync.dma_start(slot_token[:], offs)
-        for tile, pos in zip(token_slot, (pos1, pos2, pos3)):
-            nc.sync.dma_start(tile[:], pos)
         dst = w_scales[:].bitcast(I32).rearrange("p (m n) -> p m n", n=N // 4)
         for row, scales in ((W8_ROW, w8_scales), (0, w4_scales)):
             nc.sync.dma_start(dst[row:P:8], scales.bitcast(I32).rearrange("e a q n -> q (e a) n"))
@@ -185,12 +182,11 @@ def tile_moe_tk_lin_none_kernel(
             for e in range(e0, e1):
                 for a in range(a0, a1):
                     weights[e, a] = tile[:, e - e0, a - a0, :].bitcast(dtype)
-            return tile
 
-        first_weights = load_weights(0, 4, 0, 2)
+        load_weights(0, 4, 0, 2)
         scale_words = w_scales[:].bitcast(I32)
-        for row in (W8_ROW, 0):
-            for r in range(1, 4):
+        for r in range(1, 4):
+            for row in (W8_ROW, 0):
                 nc.sync.dma_start(scale_words[row + r : P : 32, :], scale_words[row + 8 * r : P : 32, :])
         load_weights(4, 8, 0, 2)
         load_weights(0, 4, 2, 4)
@@ -224,6 +220,8 @@ def tile_moe_tk_lin_none_kernel(
         move_scales(1)
         load_weights(8, 15, 3, 4)
         load_weights(8, 15, 2, 3)
+        for tile, pos in zip(token_slot, (pos1, pos2, pos3)):
+            nc.sync.dma_start(tile[:], pos)
         sums = {}
 
         def multiply(e, passes):
@@ -257,7 +255,7 @@ def tile_moe_tk_lin_none_kernel(
 
         def empty(e0, e1):
             for e in range(e0, e1):
-                copy = nc.vector.tensor_copy if e in (E - 3, E - 1) else nc.scalar.copy
+                copy = nc.vector.tensor_copy if e == E - 2 else nc.scalar.copy
                 copy(y[:, e * C : (e + 1) * C], sums[e][:])
             open_sums(e0 + BANKS, e1 + BANKS)
 
@@ -268,23 +266,11 @@ def tile_moe_tk_lin_none_kernel(
             empty(e0, e1)
 
         closes = spans(CLOSE_CUT)
-        open_sums(0, BANKS - 1)
-        spare = bank(BANK, "spare", BANKS - 1)
-        wide = slice(0, BANK)
-        for repeat in range(WARM):
-            nc.tensor.matmul_mx(
-                out=spare[:],
-                lhsT=weights[0, 0],
-                lhsT_scale=w_scales[W8_ROW:P, :N],
-                rhs=first_weights[:].rearrange("p e a b -> p (e a b)")[:, : 4 * BANK].bitcast(FP8X4),
-                rhs_scale=w_scales[W8_ROW:P, wide],
-                start=True,
-                stop=True,
-            )
-        open_sums(BANKS - 1, BANKS)
-        gather_words(PASSES - 1, 0, BANKS * C)
+        open_sums(0, BANKS)
+        gather_words(PASSES - 1, 0, FIRST * C)
         third(0, FIRST)
         empty(0, FIRST)
+        gather_words(PASSES - 1, FIRST * C, BANKS * C)
         third(FIRST, BANKS)
         close_sums(*closes[0])
         gather_words(PASSES - 1, BANKS * C, S)

@@ -24,24 +24,20 @@ PACK = 4
 K_PASS = P * PACK
 PASSES = K // K_PASS
 HALF = PASSES // 2
+LAST = PASSES - 1
 LIST_ROWS = 16
 PLANE_ROW = (4, 12, 0, 8)
-W8_ROW = 4
 GAP = 128
 WORD_START = (3 * T + GAP, 2 * T + GAP, 0, T + GAP)
 EARLY = 1792
-FIRST = 4
-CLOSE_CUT = (FIRST, 8, 12, 14, E)
-BANKS = 8
 BANK = 512
 CHUNKS = T // P
-SPARE = 2 * EARLY - T
 ALIGN = 256
-STAGE_BUFS = 8
 LOAD_CUT = ((0, 256, 512, 640), (0, 256, 512, 640), (0, 384, 640), (0, 384, 640))
 QUANT_CUT = ((0, 256, 512, 640), (0, 512, 640), (0, 512, 640), (0, 512, 640))
-SCALE_CUT = (0, 8, E)
-SCALE_WINDOW = 1536
+BANK_CUT = (0, 4, 8, 12, 14, E)
+CLOSE_CUT = (0, 8, 12, 14, E)
+W8_CUT = (0, 4, 8, 12, E)
 TURNED = 3
 VECTOR_SHARE = (256, 168, 80)
 
@@ -63,7 +59,6 @@ def tile_moe_tk_lin_none_kernel(
     with ExitStack() as ctx:
         lists = ctx.enter_context(tc.tile_pool(name="lists", bufs=1))
         keep = ctx.enter_context(tc.tile_pool(name="keep", bufs=1))
-        stage = ctx.enter_context(tc.tile_pool(name="stage", bufs=STAGE_BUFS))
         psum = ctx.enter_context(tc.psum_pool(name="psum", bufs=1))
 
         def kept(shape, dtype, name, tag=None):
@@ -75,22 +70,17 @@ def tile_moe_tk_lin_none_kernel(
         slot_token = lists.tile([P, S // LIST_ROWS], U16, name="slot_token")
         token_slot = [lists.tile([P, T // LIST_ROWS], U16, name="token_slot%d" % r) for r in range(TOP)]
 
-        def raw_tile(a, t0, t1):
-            shape = [P, PACK, t1 - t0]
-            if a > 0 and t1 == T:
-                return kept(shape, F32, "x_last%d" % a, "hold%d" % a)
-            if a == PASSES - 1:
-                return kept(shape, F32, "x_late", "late")
-            return stage.tile(shape, F32, name="x_raw%d_%d" % (a, t0), tag="stage", align_bytes=ALIGN)
-
-        x_raw = [[raw_tile(a, t0, t1) for t0, t1 in spans(LOAD_CUT[a])] for a in range(PASSES)]
+        x_raw = [
+            [kept([P, PACK, t1 - t0], F32, "x_raw%d_%d" % (a, t0)) for t0, t1 in spans(LOAD_CUT[a])]
+            for a in range(PASSES)
+        ]
         x_bf = [kept([P, T, PACK], BF16, "x_bf%d" % a) for a in range(PASSES)]
-        tok_words = kept([P, PASSES * T + GAP + SPARE], I32, "tok_words")
-        tok_scales = kept([P, SCALE_WINDOW], U8, "tok_scales")
+        tok_words = kept([P, WORD_START[0] + window_width(EARLY)], I32, "tok_words")
+        tok_scales = kept([P, window_width(S)], U8, "tok_scales")
         slot_words = {}
-        slot_scales = [kept([P, (e1 - e0) * C], U8, "slot_scales%d" % e0) for e0, e1 in spans(SCALE_CUT)]
-        last_scales = [kept([P, (e1 - e0) * C], U8, "last_scales%d" % e0) for e0, e1 in spans(SCALE_CUT)]
-        w_scales = kept([P, E * HALF * N], U8, "w_scales")
+        slot_scales = kept([P, S], U8, "slot_scales")
+        last_scales = kept([P, S], U8, "last_scales")
+        w_scales = kept([P, PASSES * E * N], U8, "w_scales")
         y = kept([P, S], F32, "y")
         identity = kept([P, P], F32, "identity")
         gate_rows = kept([P, P], F32, "gate_rows")
@@ -99,8 +89,6 @@ def tile_moe_tk_lin_none_kernel(
         make_identity(nc, identity[:])
         nc.vector.memset(gate_rows[:], 0.0)
         nc.scalar.dma_start(gate_rows[: TOP * CHUNKS, :], gate.rearrange("r n (c t) -> (r n c) t", t=P)[::P, :])
-        for plane in [w_scales] + last_scales:
-            nc.vector.memset(plane[:].bitcast(I32), 0)
         nc.vector.memset(tok_scales[:, :T].bitcast(I32), 0)
 
         for a in range(PASSES):
@@ -109,9 +97,10 @@ def tile_moe_tk_lin_none_kernel(
                 nc.sync.dma_start(raw[:], rows[:, :, t0:t1])
             if a == 0:
                 nc.sync.dma_start(slot_token[:], offs)
-        dst = w_scales[:].bitcast(I32).rearrange("p (m n) -> p m n", n=N // 4)
-        for row, scales in ((W8_ROW, w8_scales), (0, w4_scales)):
-            nc.sync.dma_start(dst[row:P:8], scales.bitcast(I32).rearrange("e a q n -> q (e a) n"))
+        scale_words = w_scales[:].bitcast(I32)
+        by_format = scale_words.rearrange("p (f m n) -> p f m n", f=2, n=N // 4)
+        for f, scales in enumerate((w8_scales, w4_scales)):
+            nc.sync.dma_start(by_format[0:P:8, f], scales.bitcast(I32).rearrange("e a q n -> q (e a) n"))
 
         def round_tokens(a, piece):
             t0, t1 = spans(LOAD_CUT[a])[piece]
@@ -134,13 +123,13 @@ def tile_moe_tk_lin_none_kernel(
 
         def gather_words(a, s0, s1, tag=None):
             first = WORD_START[a]
-            width = window_width(s1 - s0)
-            if a == HALF and tag is None:
-                width = max(width, 1024)
             words = kept([P, s1 - s0], U32, "slot_words%d_%d" % (a, s0), tag)
-            gather(words[:], tok_words[:, first : first + width].bitcast(U32), s0, s1)
+            gather(words[:], tok_words[:, first : first + window_width(s1 - s0)].bitcast(U32), s0, s1)
             for s in range(s0, s1, C):
                 slot_words[a, s // C] = words[:, s - s0 : s - s0 + C].bitcast(FP8X4)
+
+        def last_piece(a):
+            return "x_raw%d_%d" % (a, LOAD_CUT[a][-2])
 
         round_tokens(0, 0)
         quantize_tokens(0, 0)
@@ -159,8 +148,7 @@ def tile_moe_tk_lin_none_kernel(
         turned_gate = bank(P, "turned_gate", 3)
         nc.tensor.transpose(turned_gate[:], gate_rows[:], identity[:])
         nc.scalar.copy(gate_cols[:], turned_gate[:, : TOP * CHUNKS])
-        rest = T - TURNED * P
-        gates = kept([P, TOP * T], F32, "gates", "late")
+        gates = kept([P, TOP * T], F32, "gates", "x_raw%d_0" % LAST)
         for b, t0 in enumerate(range(0, TOP * T, BANK)):
             t1 = min(t0 + BANK, TOP * T)
             spread = bank(t1 - t0, "spread%d" % b, 4 + b)
@@ -175,110 +163,72 @@ def tile_moe_tk_lin_none_kernel(
 
         def load_weights(e0, e1, a0, a1):
             src, width, dtype = (w8_src, 4, FP8X4) if a0 < HALF else (w4_src, 2, FP4X4)
-            tile = stage.tile(
-                [P, e1 - e0, a1 - a0, N * width], U8, name="w%d_%d" % (e0, a0), tag="stage", align_bytes=ALIGN
-            )
+            tile = kept([P, e1 - e0, a1 - a0, N * width], U8, "w%d_%d" % (e0, a0))
             nc.sync.dma_start(tile[:].bitcast(I32), src[:, e0:e1, a0 % HALF : (a1 - 1) % HALF + 1, :])
             for e in range(e0, e1):
                 for a in range(a0, a1):
                     weights[e, a] = tile[:, e - e0, a - a0, :].bitcast(dtype)
 
-        load_weights(0, 4, 0, 2)
-        scale_words = w_scales[:].bitcast(I32)
+        w8_groups = spans(W8_CUT)
+        load_weights(*w8_groups[0], 0, HALF)
         for r in range(1, 4):
-            for row in (W8_ROW, 0):
-                nc.sync.dma_start(scale_words[row + r : P : 32, :], scale_words[row + 8 * r : P : 32, :])
-        load_weights(4, 8, 0, 2)
-        load_weights(0, 4, 2, 4)
-
-        for a in range(HALF):
-            gather_words(a, 0, EARLY)
-            for piece in range(2):
-                quantize_tokens(a + 1, piece)
-            gather_words(a, EARLY, S, "hold%d" % (a + 1))
-        for piece in range(2):
-            quantize_tokens(PASSES - 1, piece)
-        gather_words(HALF, 0, FIRST * C, "hold%d" % (PASSES - 1))
-
-        def gather_scales(half):
-            e0, e1 = spans(SCALE_CUT)[half]
-            gather(slot_scales[half][:], tok_scales[:], e0 * C, e1 * C)
-
-        def move_scales(half):
-            row = PLANE_ROW[PASSES - 1]
-            for p0, p1 in ((0, 64), (64, 68), (96, 100)):
-                nc.sync.dma_start(
-                    last_scales[half][p0:p1, :].bitcast(I32), slot_scales[half][row + p0 : row + p1, :].bitcast(I32)
-                )
-
-        gather_scales(0)
-        gather_scales(1)
-        move_scales(0)
-        load_weights(8, 12, 0, 2)
-        load_weights(4, 8, 2, 4)
-        load_weights(12, 15, 0, 2)
-        move_scales(1)
-        load_weights(8, 15, 3, 4)
-        load_weights(8, 15, 2, 3)
+            nc.sync.dma_start(scale_words[r:P:32, :], scale_words[8 * r : P : 32, :])
+        for e0, e1 in w8_groups[1:]:
+            load_weights(e0, e1, 0, HALF)
+        for a in range(HALF, PASSES):
+            load_weights(0, E, a, a + 1)
         for tile, pos in zip(token_slot, (pos1, pos2, pos3)):
             nc.sync.dma_start(tile[:], pos)
-        sums = {}
 
-        def multiply(e, passes):
-            half = 0 if e < SCALE_CUT[1] else 1
-            part = slice((e - SCALE_CUT[half]) * C, (e - SCALE_CUT[half] + 1) * C)
-            for a in passes:
-                m = HALF * e + a % HALF
-                w_row = W8_ROW if a < HALF else 0
-                if a == PASSES - 1:
-                    x_plane = last_scales[half][:, part]
-                else:
-                    x_plane = slot_scales[half][PLANE_ROW[a] : P, part]
+        gather_words(0, 0, EARLY)
+        for piece in range(2):
+            quantize_tokens(1, piece)
+        gather_words(0, EARLY, S, last_piece(1))
+        gather_words(1, 0, EARLY)
+        for a in range(HALF, PASSES):
+            for piece in range(2):
+                quantize_tokens(a, piece)
+        gather_words(1, EARLY, S, last_piece(LAST))
+        gather(slot_scales[:], tok_scales[:], 0, S)
+        row = PLANE_ROW[LAST]
+        for p0, p1 in ((0, 64), (64, 68), (96, 100)):
+            nc.sync.dma_start(last_scales[p0:p1, :].bitcast(I32), slot_scales[row + p0 : row + p1, :].bitcast(I32))
+        gather_words(HALF, 0, S)
+
+        groups = spans(BANK_CUT)
+        sums = [bank((e1 - e0) * C, "sums%d" % b, b) for b, (e0, e1) in enumerate(groups)]
+
+        def multiply(b, a):
+            e0, e1 = groups[b]
+            for e in range(e0, e1):
+                slots = slice(e * C, (e + 1) * C)
+                m = (a // HALF * E + e) * HALF + a % HALF
+                x_plane = last_scales[:, slots] if a == LAST else slot_scales[PLANE_ROW[a] : P, slots]
                 nc.tensor.matmul_mx(
-                    out=sums[e][:],
+                    out=sums[b][:, (e - e0) * C : (e - e0 + 1) * C],
                     lhsT=weights[e, a],
-                    lhsT_scale=w_scales[w_row:P, m * N : (m + 1) * N],
+                    lhsT_scale=w_scales[:, m * N : (m + 1) * N],
                     rhs=slot_words[a, e],
                     rhs_scale=x_plane,
-                    start=(a == 0),
-                    stop=(a == (PASSES - 1 if e < FIRST else HALF)),
+                    start=(a == 0 and e == e0),
+                    stop=(a == LAST and e == e1 - 1),
                 )
 
-        def open_sums(e0, e1):
-            for e in range(e0, min(e1, E)):
-                sums[e] = bank(C, "sums%d" % e, e % BANKS)
-                multiply(e, range(HALF + 1 if e < FIRST else HALF))
-
-        def third(e0, e1):
-            for e in range(e0, e1):
-                multiply(e, (PASSES - 1,))
-
-        def empty(e0, e1):
-            for e in range(e0, e1):
-                copy = nc.vector.tensor_copy if e == E - 2 else nc.scalar.copy
-                copy(y[:, e * C : (e + 1) * C], sums[e][:])
-            open_sums(e0 + BANKS, e1 + BANKS)
-
-        def close_sums(e0, e1):
-            gather_words(HALF, e0 * C, e1 * C)
-            for e in range(e0, e1):
-                multiply(e, (HALF,))
-            empty(e0, e1)
-
-        closes = spans(CLOSE_CUT)
-        open_sums(0, BANKS)
-        gather_words(PASSES - 1, 0, FIRST * C)
-        third(0, FIRST)
-        empty(0, FIRST)
-        gather_words(PASSES - 1, FIRST * C, BANKS * C)
-        third(FIRST, BANKS)
-        close_sums(*closes[0])
-        gather_words(PASSES - 1, BANKS * C, S)
-        third(BANKS, E)
-        for c0, c1 in closes[1:]:
-            close_sums(c0, c1)
+        for b in range(len(groups)):
+            for a in range(HALF):
+                multiply(b, a)
+        for b in range(len(groups)):
+            multiply(b, HALF)
+        for c0, c1 in spans(CLOSE_CUT):
+            gather_words(LAST, c0 * C, c1 * C)
+            for b, (e0, e1) in enumerate(groups):
+                if c0 <= e0 < c1:
+                    multiply(b, LAST)
+                    copy = nc.vector.tensor_copy if e1 == E else nc.scalar.copy
+                    copy(y[:, e0 * C : e1 * C], sums[b][:])
 
         head_width = TURNED * P
+        rest = T - head_width
 
         def gated(r, t0, t1):
             term = kept([P, t1 - t0], F32, "term%d_%d" % (r, t0))

@@ -33,11 +33,11 @@ EARLY = 1792
 BANK = 512
 CHUNKS = T // P
 ALIGN = 256
-LOAD_CUT = ((0, 256, 512, 640), (0, 256, 512, 640), (0, 384, 640), (0, 384, 640))
+LOAD_CUT = ((0, 256, 512, 640), (0, 256, 512, 640), (0, 384, 640), (0, 256, 512, 640))
 QUANT_CUT = ((0, 256, 512, 640), (0, 512, 640), (0, 512, 640), (0, 512, 640))
 BANK_CUT = (0, 4, 8, 12, 14, E)
 CLOSE_CUT = (0, 8, 12, 14, E)
-W8_CUT = (0, 4, 8, 12, E)
+W8_CUT = (0, 4, 8, E)
 TURNED = 3
 VECTOR_SHARE = (256, 168, 80)
 
@@ -175,10 +175,7 @@ def tile_moe_tk_lin_none_kernel(
             nc.sync.dma_start(scale_words[r:P:32, :], scale_words[8 * r : P : 32, :])
         for e0, e1 in w8_groups[1:]:
             load_weights(e0, e1, 0, HALF)
-        for a in range(HALF, PASSES):
-            load_weights(0, E, a, a + 1)
-        for tile, pos in zip(token_slot, (pos1, pos2, pos3)):
-            nc.sync.dma_start(tile[:], pos)
+        load_weights(0, E, HALF, HALF + 1)
 
         gather_words(0, 0, EARLY)
         for piece in range(2):
@@ -193,6 +190,9 @@ def tile_moe_tk_lin_none_kernel(
         row = PLANE_ROW[LAST]
         for p0, p1 in ((0, 64), (64, 68), (96, 100)):
             nc.sync.dma_start(last_scales[p0:p1, :].bitcast(I32), slot_scales[row + p0 : row + p1, :].bitcast(I32))
+        load_weights(0, E, LAST, PASSES)
+        for tile, pos in zip(token_slot, (pos1, pos2, pos3)):
+            nc.sync.dma_start(tile[:], pos)
         gather_words(HALF, 0, S)
 
         groups = spans(BANK_CUT)

@@ -39,7 +39,7 @@ BANK_CUT = (0, 4, 8, 12, 14, E)
 CLOSE_CUT = (0, 8, 12, 14, E)
 W8_CUT = (0, 4, 8, E)
 TURNED = 3
-VECTOR_SHARE = (256, 168, 80)
+VECTOR_SHARE = (256, 144, 64)
 
 
 def spans(cut):
@@ -185,7 +185,7 @@ def tile_moe_tk_lin_none_kernel(
         for a in range(HALF, PASSES):
             for piece in range(2):
                 quantize_tokens(a, piece)
-        gather_words(1, EARLY, S, last_piece(LAST))
+            gather_words(a - 1, EARLY, S, last_piece(a))
         gather(slot_scales[:], tok_scales[:], 0, S)
         row = PLANE_ROW[LAST]
         for p0, p1 in ((0, 64), (64, 68), (96, 100)):
@@ -193,7 +193,7 @@ def tile_moe_tk_lin_none_kernel(
         load_weights(0, E, LAST, PASSES)
         for tile, pos in zip(token_slot, (pos1, pos2, pos3)):
             nc.sync.dma_start(tile[:], pos)
-        gather_words(HALF, 0, S)
+        gather_words(HALF, 0, EARLY)
 
         groups = spans(BANK_CUT)
         sums = [bank((e1 - e0) * C, "sums%d" % b, b) for b, (e0, e1) in enumerate(groups)]
@@ -224,7 +224,7 @@ def tile_moe_tk_lin_none_kernel(
             for b, (e0, e1) in enumerate(groups):
                 if c0 <= e0 < c1:
                     multiply(b, LAST)
-                    copy = nc.vector.tensor_copy if e1 == E else nc.scalar.copy
+                    copy = nc.vector.tensor_copy if e1 == E - 1 else nc.scalar.copy
                     copy(y[:, e0 * C : e1 * C], sums[b][:])
 
         head_width = TURNED * P

@@ -29,13 +29,13 @@ LIST_ROWS = 16
 PLANE_ROW = (4, 12, 0, 8)
 GAP = 128
 WORD_START = (3 * T + GAP, 2 * T + GAP, 0, T + GAP)
-EARLY = 1792
+EARLY = (1792, 1664, 1664)
 BANK = 512
 CHUNKS = T // P
 ALIGN = 256
 LOAD_CUT = ((0, 256, 512, 640), (0, 256, 512, 640), (0, 384, 640), (0, 256, 512, 640))
 QUANT_CUT = ((0, 256, 512, 640), (0, 512, 640), (0, 512, 640), (0, 512, 640))
-BANK_CUT = (0, 4, 8, 12, 14, E)
+BANK_CUT = (0, 4, 8, 12, 13, 14, E)
 CLOSE_CUT = (0, 8, 12, 14, E)
 W8_CUT = (0, 4, 8, E)
 TURNED = 3
@@ -75,7 +75,7 @@ def tile_moe_tk_lin_none_kernel(
             for a in range(PASSES)
         ]
         x_bf = [kept([P, T, PACK], BF16, "x_bf%d" % a) for a in range(PASSES)]
-        tok_words = kept([P, WORD_START[0] + window_width(EARLY)], I32, "tok_words")
+        tok_words = kept([P, WORD_START[0] + window_width(EARLY[0])], I32, "tok_words")
         tok_scales = kept([P, window_width(S)], U8, "tok_scales")
         slot_words = {}
         slot_scales = kept([P, S], U8, "slot_scales")
@@ -177,15 +177,15 @@ def tile_moe_tk_lin_none_kernel(
             load_weights(e0, e1, 0, HALF)
         load_weights(0, E, HALF, HALF + 1)
 
-        gather_words(0, 0, EARLY)
+        gather_words(0, 0, EARLY[0])
         for piece in range(2):
             quantize_tokens(1, piece)
-        gather_words(0, EARLY, S, last_piece(1))
-        gather_words(1, 0, EARLY)
+        gather_words(0, EARLY[0], S, last_piece(1))
+        gather_words(1, 0, EARLY[1])
         for a in range(HALF, PASSES):
             for piece in range(2):
                 quantize_tokens(a, piece)
-            gather_words(a - 1, EARLY, S, last_piece(a))
+            gather_words(a - 1, EARLY[a - 1], S, last_piece(a))
         gather(slot_scales[:], tok_scales[:], 0, S)
         row = PLANE_ROW[LAST]
         for p0, p1 in ((0, 64), (64, 68), (96, 100)):
@@ -193,7 +193,7 @@ def tile_moe_tk_lin_none_kernel(
         load_weights(0, E, LAST, PASSES)
         for tile, pos in zip(token_slot, (pos1, pos2, pos3)):
             nc.sync.dma_start(tile[:], pos)
-        gather_words(HALF, 0, EARLY)
+        gather_words(HALF, 0, EARLY[HALF])
 
         groups = spans(BANK_CUT)
         sums = [bank((e1 - e0) * C, "sums%d" % b, b) for b, (e0, e1) in enumerate(groups)]

@@ -27,8 +27,7 @@ HALF = PASSES // 2
 LAST = PASSES - 1
 LIST_ROWS = 16
 PLANE_ROW = (4, 12, 0, 8)
-GAP = 128
-WORD_START = (3 * T + GAP, 2 * T + GAP, 0, T + GAP)
+WORD_START = (3 * T, 2 * T, 0, T)
 EARLY = (1792, 1664, 1664)
 BANK = 512
 CHUNKS = T // P
@@ -37,7 +36,7 @@ LOAD_CUT = ((0, 256, 512, 640), (0, 256, 512, 640), (0, 384, 640), (0, 256, 512,
 QUANT_CUT = ((0, 256, 512, 640), (0, 512, 640), (0, 512, 640), (0, 512, 640))
 BANK_CUT = (0, 4, 8, 12, 13, 14, E)
 CLOSE_CUT = (0, 8, 12, 14, E)
-W8_CUT = (0, 4, 8, E)
+W8_CUT = (0, 6, E)
 TURNED = 3
 VECTOR_SHARE = (256, 144, 64)
 
@@ -89,7 +88,6 @@ def tile_moe_tk_lin_none_kernel(
         make_identity(nc, identity[:])
         nc.vector.memset(gate_rows[:], 0.0)
         nc.scalar.dma_start(gate_rows[: TOP * CHUNKS, :], gate.rearrange("r n (c t) -> (r n c) t", t=P)[::P, :])
-        nc.vector.memset(tok_scales[:, :T].bitcast(I32), 0)
 
         for a in range(PASSES):
             rows = xT[a * K_PASS : (a + 1) * K_PASS, :].rearrange("(p j) t -> p j t", j=PACK)
@@ -188,8 +186,8 @@ def tile_moe_tk_lin_none_kernel(
             gather_words(a - 1, EARLY[a - 1], S, last_piece(a))
         gather(slot_scales[:], tok_scales[:], 0, S)
         row = PLANE_ROW[LAST]
-        for p0, p1 in ((0, 64), (64, 68), (96, 100)):
-            nc.sync.dma_start(last_scales[p0:p1, :].bitcast(I32), slot_scales[row + p0 : row + p1, :].bitcast(I32))
+        for q in range(0, P, 32):
+            nc.sync.dma_start(last_scales[q : q + 4, :].bitcast(I32), slot_scales[row + q : row + q + 4, :].bitcast(I32))
         load_weights(0, E, LAST, PASSES)
         for tile, pos in zip(token_slot, (pos1, pos2, pos3)):
             nc.sync.dma_start(tile[:], pos)

@@ -18,6 +18,7 @@ FP8X4 = mybir.dt.float8_e4m3fn_x4
 FP4X4 = mybir.dt.float4_e2m1fn_x4
 MULT = mybir.AluOpType.mult
 ADD = mybir.AluOpType.add
+COPY = mybir.ActivationFunctionType.Copy
 
 P = 128
 PACK = 4
@@ -153,7 +154,7 @@ def tile_moe_tk_lin_none_kernel(
             for t in range(t0, t1, P):
                 column = gate_col(*divmod(t // P, CHUNKS))
                 nc.tensor.transpose(spread[:, t - t0 : t - t0 + P], column.to_broadcast([P, P]), identity[:])
-            nc.scalar.copy(gates[:, t0:t1], spread[:])
+            nc.scalar.activation(gates[:, t0:t1], spread[:], COPY)
 
         w8_src = w8_words.rearrange("e a p n t -> p e a (n t)").bitcast(I32)
         w4_src = w4_words.rearrange("e a p b -> p e a b").bitcast(I32)
@@ -228,14 +229,31 @@ def tile_moe_tk_lin_none_kernel(
         head_width = TURNED * P
         rest = T - head_width
 
+        def offsets(r, t0, t1):
+            return token_slot[r][:, t0 // LIST_ROWS : t1 // LIST_ROWS]
+
         def gated(r, t0, t1):
             term = kept([P, t1 - t0], F32, "term%d_%d" % (r, t0))
-            offsets = token_slot[r][:, t0 // LIST_ROWS : t1 // LIST_ROWS]
-            nc.vector.tensor_tensor(term[:], y[:].indirect(offsets), gates[:, r * T + t0 : r * T + t1], MULT)
+            nc.vector.tensor_tensor(term[:], y[:].indirect(offsets(r, t0, t1)), gates[:, r * T + t0 : r * T + t1], MULT)
             return term
 
-        head_terms = [gated(r, 0, head_width) for r in range(TOP)]
-        terms = [gated(r, head_width, T) for r in range(TOP)]
+        def fetch(dst, r, t0, t1):
+            nc.scalar.activation(dst, y[:].indirect(offsets(r, t0, t1)), COPY)
+
+        plain_head = kept([P, head_width], F32, "plain_head")
+        plain_rest = kept([P, 2, rest], F32, "plain_rest")
+        fetch(plain_head[:], 2, 0, head_width)
+        for r in (1, 2):
+            fetch(plain_rest[:, r - 1, :], r, head_width, T)
+
+        head_terms = [gated(r, 0, head_width) for r in range(2)]
+        third = kept([P, head_width], F32, "third")
+        nc.vector.tensor_tensor(third[:], plain_head[:], gates[:, 2 * T : 2 * T + head_width], MULT)
+        head_terms.append(third)
+        pair = kept([P, 2, rest], F32, "pair")
+        by_choice = gates[:].rearrange("p (r t) -> p r t", r=TOP)
+        nc.vector.tensor_tensor(pair[:], plain_rest[:], by_choice[:, 1:, head_width:], MULT)
+        first = gated(0, head_width, T)
         flipped = [bank(P, "flipped%d" % c, c) for c in range(TURNED)]
         for r in range(TOP):
             for c in range(TURNED):
@@ -260,6 +278,6 @@ def tile_moe_tk_lin_none_kernel(
 
         partial = kept([P, rest], F32, "partial")
         tail = kept([P, rest], F32, "tail")
-        nc.vector.tensor_tensor(partial[:], terms[0][:], terms[1][:], ADD)
-        nc.vector.tensor_tensor(tail[:], partial[:], terms[2][:], ADD)
+        nc.vector.tensor_tensor(partial[:], pair[:, 0, :], pair[:, 1, :], ADD)
+        nc.vector.tensor_tensor(tail[:], partial[:], first[:], ADD)
         nc.sync.dma_start(out[:, head_width:], tail[:])

@@ -38,7 +38,8 @@ QUANT_CUT = ((0, 256, 512, 640), (0, 512, 640), (0, 512, 640), (0, 512, 640))
 BANK_CUT = (0, 4, 8, 12, 13, 14, E)
 CLOSE_CUT = (0, 8, 12, 14, E)
 W8_CUT = (0, 6, E)
-TURNED = 3
+TURNED = 2
+ADD_CUT = (256, 512, 640)
 VECTOR_SHARE = (256, 144, 64)
 
 
@@ -226,34 +227,39 @@ def tile_moe_tk_lin_none_kernel(
                     copy = nc.vector.tensor_copy if e1 == E - 1 else nc.scalar.copy
                     copy(y[:, e0 * C : e1 * C], sums[b][:])
 
-        head_width = TURNED * P
-        rest = T - head_width
+        by_choice = gates[:].rearrange("p (r t) -> p r t", r=TOP)
 
         def offsets(r, t0, t1):
             return token_slot[r][:, t0 // LIST_ROWS : t1 // LIST_ROWS]
 
         def gated(r, t0, t1):
             term = kept([P, t1 - t0], F32, "term%d_%d" % (r, t0))
-            nc.vector.tensor_tensor(term[:], y[:].indirect(offsets(r, t0, t1)), gates[:, r * T + t0 : r * T + t1], MULT)
+            nc.vector.tensor_tensor(term[:], y[:].indirect(offsets(r, t0, t1)), by_choice[:, r, t0:t1], MULT)
             return term
 
-        def fetch(dst, r, t0, t1):
-            nc.scalar.activation(dst, y[:].indirect(offsets(r, t0, t1)), COPY)
+        def fetch(r0, t0, t1):
+            plain = kept([P, TOP - r0, t1 - t0], F32, "plain%d" % t0)
+            for r in range(r0, TOP):
+                nc.scalar.activation(plain[:, r - r0, :], y[:].indirect(offsets(r, t0, t1)), COPY)
+            return plain
 
-        plain_head = kept([P, head_width], F32, "plain_head")
-        plain_rest = kept([P, 2, rest], F32, "plain_rest")
-        fetch(plain_head[:], 2, 0, head_width)
-        for r in (1, 2):
-            fetch(plain_rest[:, r - 1, :], r, head_width, T)
+        def weigh(plain, r0, t0, t1):
+            terms = kept([P, TOP - r0, t1 - t0], F32, "weighed%d" % t0)
+            nc.vector.tensor_tensor(terms[:], plain[:], by_choice[:, r0:, t0:t1], MULT)
+            return terms
 
-        head_terms = [gated(r, 0, head_width) for r in range(2)]
-        third = kept([P, head_width], F32, "third")
-        nc.vector.tensor_tensor(third[:], plain_head[:], gates[:, 2 * T : 2 * T + head_width], MULT)
-        head_terms.append(third)
-        pair = kept([P, 2, rest], F32, "pair")
-        by_choice = gates[:].rearrange("p (r t) -> p r t", r=TOP)
-        nc.vector.tensor_tensor(pair[:], plain_rest[:], by_choice[:, 1:, head_width:], MULT)
-        first = gated(0, head_width, T)
+        def add(name, in0, in1):
+            total = kept(list(in0.shape), F32, name)
+            nc.vector.tensor_tensor(total[:], in0, in1, ADD)
+            return total
+
+        head_width = TURNED * P
+        added = spans(ADD_CUT)
+        plain_head = fetch(2, 0, head_width)
+        plains = [fetch(1, t0, t1) for t0, t1 in added]
+
+        head_terms = [gated(r, 0, head_width)[:] for r in range(2)]
+        head_terms.append(weigh(plain_head, 2, 0, head_width)[:, 0, :])
         flipped = [bank(P, "flipped%d" % c, c) for c in range(TURNED)]
         for r in range(TOP):
             for c in range(TURNED):
@@ -272,12 +278,11 @@ def tile_moe_tk_lin_none_kernel(
             back = bank(P, "back%d" % c, TURNED + c)
             nc.tensor.transpose(back[:], flipped_sb[:], identity[:])
             nc.scalar.copy(head[:, c * P : (c + 1) * P], back[:])
-            if c > 0:
-                t0 = 0 if c == 1 else c * P
-                nc.sync.dma_start(out[:, t0 : (c + 1) * P], head[:, t0 : (c + 1) * P])
+        nc.sync.dma_start(out[:, :head_width], head[:])
 
-        partial = kept([P, rest], F32, "partial")
-        tail = kept([P, rest], F32, "tail")
-        nc.vector.tensor_tensor(partial[:], pair[:, 0, :], pair[:, 1, :], ADD)
-        nc.vector.tensor_tensor(tail[:], partial[:], first[:], ADD)
-        nc.sync.dma_start(out[:, head_width:], tail[:])
+        first = gated(0, head_width, T)
+        pairs = [weigh(plain, 1, t0, t1) for plain, (t0, t1) in zip(plains, added)]
+        partials = [add("partial%d" % g, pair[:, 0, :], pair[:, 1, :]) for g, pair in enumerate(pairs)]
+        for partial, (t0, t1) in zip(partials, added):
+            total = add("total%d" % t0, partial[:], first[:, t0 - head_width : t1 - head_width])
+            nc.sync.dma_start(out[:, t0:t1], total[:])

@@ -39,7 +39,7 @@ BANK_CUT = (0, 4, 8, 12, 13, 14, E)
 CLOSE_CUT = (0, 8, 12, 14, E)
 W8_CUT = (0, 6, E)
 TURNED = 2
-ADD_CUT = (256, 512, 640)
+ADD_CUT = (256, 448, 640)
 VECTOR_SHARE = (256, 144, 64)
 
 
@@ -148,14 +148,14 @@ def tile_moe_tk_lin_none_kernel(
         turned_gate = bank(P, "turned_gate", 3)
         nc.tensor.transpose(turned_gate[:], gate_rows[:], identity[:])
         nc.scalar.copy(gate_cols[:], turned_gate[:, : TOP * CHUNKS])
-        gates = kept([P, TOP * T], F32, "gates", "x_raw%d_0" % LAST)
-        for b, t0 in enumerate(range(0, TOP * T, BANK)):
-            t1 = min(t0 + BANK, TOP * T)
-            spread = bank(t1 - t0, "spread%d" % b, 4 + b)
-            for t in range(t0, t1, P):
-                column = gate_col(*divmod(t // P, CHUNKS))
-                nc.tensor.transpose(spread[:, t - t0 : t - t0 + P], column.to_broadcast([P, P]), identity[:])
-            nc.scalar.activation(gates[:, t0:t1], spread[:], COPY)
+        head_width = TURNED * P
+        gates = kept([P, TOP, T - head_width], F32, "gates", "x_raw%d_0" % LAST)
+        for r in range(TOP):
+            spread = bank(T - head_width, "spread%d" % r, 4 + r)
+            for c in range(TURNED, CHUNKS):
+                columns = spread[:, (c - TURNED) * P : (c - TURNED + 1) * P]
+                nc.tensor.transpose(columns, gate_col(r, c).to_broadcast([P, P]), identity[:])
+            nc.scalar.activation(gates[:, r, :], spread[:], COPY)
 
         w8_src = w8_words.rearrange("e a p n t -> p e a (n t)").bitcast(I32)
         w4_src = w4_words.rearrange("e a p b -> p e a b").bitcast(I32)
@@ -227,62 +227,42 @@ def tile_moe_tk_lin_none_kernel(
                     copy = nc.vector.tensor_copy if e1 == E - 1 else nc.scalar.copy
                     copy(y[:, e0 * C : e1 * C], sums[b][:])
 
-        by_choice = gates[:].rearrange("p (r t) -> p r t", r=TOP)
-
         def offsets(r, t0, t1):
             return token_slot[r][:, t0 // LIST_ROWS : t1 // LIST_ROWS]
 
-        def gated(r, t0, t1):
-            term = kept([P, t1 - t0], F32, "term%d_%d" % (r, t0))
-            nc.vector.tensor_tensor(term[:], y[:].indirect(offsets(r, t0, t1)), by_choice[:, r, t0:t1], MULT)
-            return term
+        plain = [kept([P, head_width], F32, "plain%d" % r) for r in range(TOP)]
+        for r in range(TOP):
+            nc.scalar.activation(plain[r][:], y[:].indirect(offsets(r, 0, head_width)), COPY)
+        terms = [kept([P, T - head_width], F32, "term%d" % r) for r in range(TOP)]
+        for r in range(TOP):
+            nc.vector.tensor_tensor(terms[r][:], y[:].indirect(offsets(r, head_width, T)), gates[:, r, :], MULT)
 
-        def fetch(r0, t0, t1):
-            plain = kept([P, TOP - r0, t1 - t0], F32, "plain%d" % t0)
-            for r in range(r0, TOP):
-                nc.scalar.activation(plain[:, r - r0, :], y[:].indirect(offsets(r, t0, t1)), COPY)
-            return plain
-
-        def weigh(plain, r0, t0, t1):
-            terms = kept([P, TOP - r0, t1 - t0], F32, "weighed%d" % t0)
-            nc.vector.tensor_tensor(terms[:], plain[:], by_choice[:, r0:, t0:t1], MULT)
-            return terms
+        flipped = {}
+        for r in range(TOP):
+            for c in range(TURNED):
+                flipped[r, c] = bank(P, "flipped%d_%d" % (r, c), r * TURNED + c)
+                nc.tensor.transpose(flipped[r, c][:], plain[r][:, c * P : (c + 1) * P], identity[:])
+        back = [bank(P, "back%d" % c, TOP * TURNED + c) for c in range(TURNED)]
+        for r in range(TOP):
+            for c in range(TURNED):
+                weighed = kept([P, P], F32, "weighed%d_%d" % (r, c))
+                nc.scalar.activation(weighed[:], flipped[r, c][:], COPY, scale=gate_col(r, c))
+                nc.tensor.matmul(
+                    back[c][:], weighed[:], identity[:], start=(r == 0), stop=(r == TOP - 1), is_transpose=True
+                )
 
         def add(name, in0, in1):
             total = kept(list(in0.shape), F32, name)
             nc.vector.tensor_tensor(total[:], in0, in1, ADD)
             return total
 
-        head_width = TURNED * P
-        added = spans(ADD_CUT)
-        plain_head = fetch(2, 0, head_width)
-        plains = [fetch(1, t0, t1) for t0, t1 in added]
+        added = [slice(t0 - head_width, t1 - head_width) for t0, t1 in spans(ADD_CUT)]
+        partials = [add("partial%d" % g, terms[0][:, cols], terms[1][:, cols]) for g, cols in enumerate(added)]
+        for partial, cols, (t0, t1) in zip(partials, added, spans(ADD_CUT)):
+            total = add("total%d" % t0, partial[:], terms[2][:, cols])
+            nc.sync.dma_start(out[:, t0:t1], total[:])
 
-        head_terms = [gated(r, 0, head_width)[:] for r in range(2)]
-        head_terms.append(weigh(plain_head, 2, 0, head_width)[:, 0, :])
-        flipped = [bank(P, "flipped%d" % c, c) for c in range(TURNED)]
-        for r in range(TOP):
-            for c in range(TURNED):
-                nc.tensor.matmul(
-                    flipped[c][:],
-                    head_terms[r][:, c * P : (c + 1) * P],
-                    identity[:],
-                    start=(r == 0),
-                    stop=(r == TOP - 1),
-                    is_transpose=True,
-                )
         head = kept([P, head_width], F32, "head")
         for c in range(TURNED):
-            flipped_sb = kept([P, P], F32, "flipped_sb%d" % c)
-            nc.scalar.copy(flipped_sb[:], flipped[c][:])
-            back = bank(P, "back%d" % c, TURNED + c)
-            nc.tensor.transpose(back[:], flipped_sb[:], identity[:])
-            nc.scalar.copy(head[:, c * P : (c + 1) * P], back[:])
+            nc.scalar.copy(head[:, c * P : (c + 1) * P], back[c][:])
         nc.sync.dma_start(out[:, :head_width], head[:])
-
-        first = gated(0, head_width, T)
-        pairs = [weigh(plain, 1, t0, t1) for plain, (t0, t1) in zip(plains, added)]
-        partials = [add("partial%d" % g, pair[:, 0, :], pair[:, 1, :]) for g, pair in enumerate(pairs)]
-        for partial, (t0, t1) in zip(partials, added):
-            total = add("total%d" % t0, partial[:], first[:, t0 - head_width : t1 - head_width])
-            nc.sync.dma_start(out[:, t0:t1], total[:])

@@ -175,7 +175,8 @@ def tile_moe_tk_lin_none_kernel(
             nc.sync.dma_start(scale_words[r:P:32, :], scale_words[8 * r : P : 32, :])
         for e0, e1 in w8_groups[1:]:
             load_weights(e0, e1, 0, HALF)
-        load_weights(0, E, HALF, HALF + 1)
+        for a in range(HALF, PASSES):
+            load_weights(0, E, a, a + 1)
 
         gather_words(0, 0, EARLY[0])
         for piece in range(2):
@@ -190,7 +191,6 @@ def tile_moe_tk_lin_none_kernel(
         row = PLANE_ROW[LAST]
         for q in range(0, P, 32):
             nc.sync.dma_start(last_scales[q : q + 4, :].bitcast(I32), slot_scales[row + q : row + q + 4, :].bitcast(I32))
-        load_weights(0, E, LAST, PASSES)
         for tile, pos in zip(token_slot, (pos1, pos2, pos3)):
             nc.sync.dma_start(tile[:], pos)
         gather_words(HALF, 0, EARLY[HALF])

@@ -27,17 +27,19 @@ PASSES = K // K_PASS
 HALF = PASSES // 2
 LAST = PASSES - 1
 LIST_ROWS = 16
-PLANE_ROW = (4, 12, 0, 8)
-WORD_START = (3 * T, 2 * T, 0, T)
+ORDER = (2, 0, 3, 1)
+MOVED = 3
+PLANE_ROW = (12, 4, 0, 8)
+WORD_START = (2 * T, T, 3 * T, 0)
 EARLY = (1792, 1664, 1664)
 BANK = 512
 CHUNKS = T // P
 ALIGN = 256
-LOAD_CUT = ((0, 256, 512, 640), (0, 256, 512, 640), (0, 384, 640), (0, 256, 512, 640))
-QUANT_CUT = ((0, 256, 512, 640), (0, 512, 640), (0, 512, 640), (0, 512, 640))
+LOAD_CUT = ((0, 384, 640), (0, 512, 640), (0, 256, 512, 640), (0, 384, 640))
+QUANT_CUT = ((0, 512, 640), (0, 512, 640), (0, 256, 512, 640), (0, 512, 640))
 BANK_CUT = (0, 4, 8, 12, 13, 14, E)
 CLOSE_CUT = (0, 8, 12, 14, E)
-W8_CUT = (0, 6, E)
+LAST_CUT = (0, 8, E)
 TURNED = 2
 ADD_CUT = (256, 448, 640)
 VECTOR_SHARE = (256, 144, 64)
@@ -76,7 +78,7 @@ def tile_moe_tk_lin_none_kernel(
             for a in range(PASSES)
         ]
         x_bf = [kept([P, T, PACK], BF16, "x_bf%d" % a) for a in range(PASSES)]
-        tok_words = kept([P, WORD_START[0] + window_width(EARLY[0])], I32, "tok_words")
+        tok_words = kept([P, WORD_START[ORDER[0]] + window_width(EARLY[0])], I32, "tok_words")
         tok_scales = kept([P, window_width(S)], U8, "tok_scales")
         slot_words = {}
         slot_scales = kept([P, S], U8, "slot_scales")
@@ -89,14 +91,15 @@ def tile_moe_tk_lin_none_kernel(
 
         make_identity(nc, identity[:])
         nc.vector.memset(gate_rows[:], 0.0)
-        nc.scalar.dma_start(gate_rows[: TOP * CHUNKS, :], gate.rearrange("r n (c t) -> (r n c) t", t=P)[::P, :])
 
-        for a in range(PASSES):
+        for a in ORDER:
             rows = xT[a * K_PASS : (a + 1) * K_PASS, :].rearrange("(p j) t -> p j t", j=PACK)
             for raw, (t0, t1) in zip(x_raw[a], spans(LOAD_CUT[a])):
                 nc.sync.dma_start(raw[:], rows[:, :, t0:t1])
-            if a == 0:
+            if a == ORDER[0]:
                 nc.sync.dma_start(slot_token[:], offs)
+            if a == ORDER[1]:
+                nc.sync.dma_start(gate_rows[: TOP * CHUNKS, :], gate.rearrange("r n (c t) -> (r n c) t", t=P)[::P, :])
         scale_words = w_scales[:].bitcast(I32)
         by_format = scale_words.rearrange("p (f m n) -> p f m n", f=2, n=N // 4)
         for f, scales in enumerate((w8_scales, w4_scales)):
@@ -104,7 +107,7 @@ def tile_moe_tk_lin_none_kernel(
 
         def round_tokens(a, piece):
             t0, t1 = spans(LOAD_CUT[a])[piece]
-            split = VECTOR_SHARE[piece] if a == 0 else 0
+            split = VECTOR_SHARE[piece] if a == ORDER[0] else 0
             for copy, c0, c1 in ((nc.vector.tensor_copy, 0, split), (nc.scalar.copy, split, t1 - t0)):
                 if c1 > c0:
                     dst = x_bf[a][:, t0 + c0 : t0 + c1, :].rearrange("p (c i) j -> p c j i", i=4)
@@ -131,13 +134,13 @@ def tile_moe_tk_lin_none_kernel(
         def last_piece(a):
             return "x_raw%d_%d" % (a, LOAD_CUT[a][-2])
 
-        round_tokens(0, 0)
-        quantize_tokens(0, 0)
-        round_tokens(0, 1)
-        round_tokens(0, 2)
-        quantize_tokens(0, 1)
-        quantize_tokens(0, 2)
-        for a in range(1, PASSES):
+        round_tokens(ORDER[0], 0)
+        quantize_tokens(ORDER[0], 0)
+        round_tokens(ORDER[0], 1)
+        round_tokens(ORDER[0], 2)
+        quantize_tokens(ORDER[0], 1)
+        quantize_tokens(ORDER[0], 2)
+        for a in ORDER[1:]:
             for piece in range(len(x_raw[a])):
                 round_tokens(a, piece)
 
@@ -149,7 +152,7 @@ def tile_moe_tk_lin_none_kernel(
         nc.tensor.transpose(turned_gate[:], gate_rows[:], identity[:])
         nc.scalar.copy(gate_cols[:], turned_gate[:, : TOP * CHUNKS])
         head_width = TURNED * P
-        gates = kept([P, TOP, T - head_width], F32, "gates", "x_raw%d_0" % LAST)
+        gates = kept([P, TOP, T - head_width], F32, "gates", "x_raw%d_0" % ORDER[LAST])
         for r in range(TOP):
             spread = bank(T - head_width, "spread%d" % r, 4 + r)
             for c in range(TURNED, CHUNKS):
@@ -169,31 +172,30 @@ def tile_moe_tk_lin_none_kernel(
                 for a in range(a0, a1):
                     weights[e, a] = tile[:, e - e0, a - a0, :].bitcast(dtype)
 
-        w8_groups = spans(W8_CUT)
-        load_weights(*w8_groups[0], 0, HALF)
+        load_weights(0, E, ORDER[0], ORDER[0] + 1)
         for r in range(1, 4):
             nc.sync.dma_start(scale_words[r:P:32, :], scale_words[8 * r : P : 32, :])
-        for e0, e1 in w8_groups[1:]:
-            load_weights(e0, e1, 0, HALF)
-        for a in range(HALF, PASSES):
+        for a in ORDER[1:LAST]:
             load_weights(0, E, a, a + 1)
+        for e0, e1 in spans(LAST_CUT):
+            load_weights(e0, e1, ORDER[LAST], ORDER[LAST] + 1)
 
-        gather_words(0, 0, EARLY[0])
+        gather_words(ORDER[0], 0, EARLY[0])
         for piece in range(2):
-            quantize_tokens(1, piece)
-        gather_words(0, EARLY[0], S, last_piece(1))
-        gather_words(1, 0, EARLY[1])
-        for a in range(HALF, PASSES):
+            quantize_tokens(ORDER[1], piece)
+        gather_words(ORDER[0], EARLY[0], S, last_piece(ORDER[1]))
+        gather_words(ORDER[1], 0, EARLY[1])
+        for i in range(HALF, PASSES):
             for piece in range(2):
-                quantize_tokens(a, piece)
-            gather_words(a - 1, EARLY[a - 1], S, last_piece(a))
+                quantize_tokens(ORDER[i], piece)
+            gather_words(ORDER[i - 1], EARLY[i - 1], S, last_piece(ORDER[i]))
         gather(slot_scales[:], tok_scales[:], 0, S)
-        row = PLANE_ROW[LAST]
+        row = PLANE_ROW[MOVED]
         for q in range(0, P, 32):
             nc.sync.dma_start(last_scales[q : q + 4, :].bitcast(I32), slot_scales[row + q : row + q + 4, :].bitcast(I32))
         for tile, pos in zip(token_slot, (pos1, pos2, pos3)):
             nc.sync.dma_start(tile[:], pos)
-        gather_words(HALF, 0, EARLY[HALF])
+        gather_words(ORDER[HALF], 0, EARLY[HALF])
 
         groups = spans(BANK_CUT)
         sums = [bank((e1 - e0) * C, "sums%d" % b, b) for b, (e0, e1) in enumerate(groups)]
@@ -203,27 +205,27 @@ def tile_moe_tk_lin_none_kernel(
             for e in range(e0, e1):
                 slots = slice(e * C, (e + 1) * C)
                 m = (a // HALF * E + e) * HALF + a % HALF
-                x_plane = last_scales[:, slots] if a == LAST else slot_scales[PLANE_ROW[a] : P, slots]
+                x_plane = last_scales[:, slots] if a == MOVED else slot_scales[PLANE_ROW[a] : P, slots]
                 nc.tensor.matmul_mx(
                     out=sums[b][:, (e - e0) * C : (e - e0 + 1) * C],
                     lhsT=weights[e, a],
                     lhsT_scale=w_scales[:, m * N : (m + 1) * N],
                     rhs=slot_words[a, e],
                     rhs_scale=x_plane,
-                    start=(a == 0 and e == e0),
-                    stop=(a == LAST and e == e1 - 1),
+                    start=(a == ORDER[0] and e == e0),
+                    stop=(a == ORDER[LAST] and e == e1 - 1),
                 )
 
         for b in range(len(groups)):
-            for a in range(HALF):
+            for a in ORDER[:HALF]:
                 multiply(b, a)
         for b in range(len(groups)):
-            multiply(b, HALF)
+            multiply(b, ORDER[HALF])
         for c0, c1 in spans(CLOSE_CUT):
-            gather_words(LAST, c0 * C, c1 * C)
+            gather_words(ORDER[LAST], c0 * C, c1 * C)
             for b, (e0, e1) in enumerate(groups):
                 if c0 <= e0 < c1:
-                    multiply(b, LAST)
+                    multiply(b, ORDER[LAST])
                     copy = nc.vector.tensor_copy if e1 == E - 1 else nc.scalar.copy
                     copy(y[:, e0 * C : e1 * C], sums[b][:])
 
@@ -243,8 +245,8 @@ def tile_moe_tk_lin_none_kernel(
                 flipped[r, c] = bank(P, "flipped%d_%d" % (r, c), r * TURNED + c)
                 nc.tensor.transpose(flipped[r, c][:], plain[r][:, c * P : (c + 1) * P], identity[:])
         back = [bank(P, "back%d" % c, TOP * TURNED + c) for c in range(TURNED)]
-        for r in range(TOP):
-            for c in range(TURNED):
+        for c in range(TURNED):
+            for r in range(TOP):
                 weighed = kept([P, P], F32, "weighed%d_%d" % (r, c))
                 nc.scalar.activation(weighed[:], flipped[r, c][:], COPY, scale=gate_col(r, c))
                 nc.tensor.matmul(
@@ -262,7 +264,7 @@ def tile_moe_tk_lin_none_kernel(
             total = add("total%d" % t0, partial[:], terms[2][:, cols])
             nc.sync.dma_start(out[:, t0:t1], total[:])
 
-        head = kept([P, head_width], F32, "head")
         for c in range(TURNED):
-            nc.scalar.copy(head[:, c * P : (c + 1) * P], back[c][:])
-        nc.sync.dma_start(out[:, :head_width], head[:])
+            head = kept([P, P], F32, "head%d" % c)
+            nc.scalar.copy(head[:], back[c][:])
+            nc.sync.dma_start(out[:, c * P : (c + 1) * P], head[:])

from contextlib import ExitStack

import concourse.mybir as mybir
from concourse.masks import make_identity

K, T, E, C, N = 2048, 640, 15, 128, 128
TOP = 3
S = E * C
FLOPS = 2 * K * N * S

F32 = mybir.dt.float32
BF16 = mybir.dt.bfloat16
I32 = mybir.dt.int32
U32 = mybir.dt.uint32
U16 = mybir.dt.uint16
U8 = mybir.dt.uint8
FP8X4 = mybir.dt.float8_e4m3fn_x4
FP4X4 = mybir.dt.float4_e2m1fn_x4
MULT = mybir.AluOpType.mult
ADD = mybir.AluOpType.add
COPY = mybir.ActivationFunctionType.Copy

P = 128
PACK = 4
K_PASS = P * PACK
PASSES = K // K_PASS
HALF = PASSES // 2
LAST = PASSES - 1
LIST_ROWS = 16
ORDER = (2, 0, 3, 1)
MOVED = 3
PLANE_ROW = (12, 4, 0, 8)
WORD_START = (2 * T, T, 3 * T, 0)
EARLY = (1792, 1664, 1664)
BANK = 512
CHUNKS = T // P
ALIGN = 256
LOAD_CUT = ((0, 384, 640), (0, 512, 640), (0, 256, 512, 640), (0, 384, 640))
QUANT_CUT = ((0, 512, 640), (0, 512, 640), (0, 256, 512, 640), (0, 512, 640))
BANK_CUT = (0, 4, 8, 12, 13, 14, E)
CLOSE_CUT = (0, 8, 12, 14, E)
LAST_CUT = (0, 8, E)
TURNED = 2
ADD_CUT = (256, 448, 640)
VECTOR_SHARE = (256, 144, 64)


def spans(cut):
    return list(zip(cut[:-1], cut[1:]))


def window_width(entries):
    if entries > 1536:
        return 2 * entries
    return max(T, min(3 * entries // 2, 2048))


def tile_moe_tk_lin_none_kernel(
    tc, xT, w8_words, w8_scales, w4_words, w4_scales, gate, offs, pos1, pos2, pos3, out
):
    nc = tc.nc
    with ExitStack() as ctx:
        lists = ctx.enter_context(tc.tile_pool(name="lists", bufs=1))
        keep = ctx.enter_context(tc.tile_pool(name="keep", bufs=1))
        psum = ctx.enter_context(tc.psum_pool(name="psum", bufs=1))

        def kept(shape, dtype, name, tag=None):
            return keep.tile(shape, dtype, name=name, tag=tag or name, align_bytes=ALIGN)

        def bank(width, name, b):
            return psum.tile([P, width], F32, name=name, tag="bank%d" % b)

        slot_token = lists.tile([P, S // LIST_ROWS], U16, name="slot_token")
        token_slot = [lists.tile([P, T // LIST_ROWS], U16, name="token_slot%d" % r) for r in range(TOP)]

        x_raw = [
            [kept([P, PACK, t1 - t0], F32, "x_raw%d_%d" % (a, t0)) for t0, t1 in spans(LOAD_CUT[a])]
            for a in range(PASSES)
        ]
        x_bf = [kept([P, T, PACK], BF16, "x_bf%d" % a) for a in range(PASSES)]
        tok_words = kept([P, WORD_START[ORDER[0]] + window_width(EARLY[0])], I32, "tok_words")
        tok_scales = kept([P, window_width(S)], U8, "tok_scales")
        slot_words = {}
        slot_scales = kept([P, S], U8, "slot_scales")
        last_scales = kept([P, S], U8, "last_scales")
        w_scales = kept([P, PASSES * E * N], U8, "w_scales")
        y = kept([P, S], F32, "y")
        identity = kept([P, P], F32, "identity")
        gate_rows = kept([P, P], F32, "gate_rows")
        gate_cols = kept([P, TOP * CHUNKS], F32, "gate_cols")

        make_identity(nc, identity[:])
        nc.vector.memset(gate_rows[:], 0.0)

        for a in ORDER:
            rows = xT[a * K_PASS : (a + 1) * K_PASS, :].rearrange("(p j) t -> p j t", j=PACK)
            for raw, (t0, t1) in zip(x_raw[a], spans(LOAD_CUT[a])):
                nc.sync.dma_start(raw[:], rows[:, :, t0:t1])
            if a == ORDER[0]:
                nc.sync.dma_start(slot_token[:], offs)
            if a == ORDER[1]:
                nc.sync.dma_start(gate_rows[: TOP * CHUNKS, :], gate.rearrange("r n (c t) -> (r n c) t", t=P)[::P, :])
        scale_words = w_scales[:].bitcast(I32)
        by_format = scale_words.rearrange("p (f m n) -> p f m n", f=2, n=N // 4)
        for f, scales in enumerate((w8_scales, w4_scales)):
            nc.sync.dma_start(by_format[0:P:8, f], scales.bitcast(I32).rearrange("e a q n -> q (e a) n"))

        def round_tokens(a, piece):
            t0, t1 = spans(LOAD_CUT[a])[piece]
            split = VECTOR_SHARE[piece] if a == ORDER[0] else 0
            for copy, c0, c1 in ((nc.vector.tensor_copy, 0, split), (nc.scalar.copy, split, t1 - t0)):
                if c1 > c0:
                    dst = x_bf[a][:, t0 + c0 : t0 + c1, :].rearrange("p (c i) j -> p c j i", i=4)
                    copy(dst, x_raw[a][piece][:, :, c0:c1].rearrange("p j (c i) -> p c j i", i=4))

        def quantize_tokens(a, piece):
            t0, t1 = spans(QUANT_CUT[a])[piece]
            nc.vector.quantize_mx(
                out=tok_words[:, WORD_START[a] + t0 : WORD_START[a] + t1].bitcast(FP8X4),
                scales=tok_scales[PLANE_ROW[a] : P, t0:t1],
                in_=x_bf[a][:, t0:t1, :].rearrange("p t j -> p (t j)"),
            )

        def gather(dst, window, s0, s1):
            nc.vector.tensor_copy(dst, window.indirect(slot_token[:, s0 // LIST_ROWS : s1 // LIST_ROWS]))

        def gather_words(a, s0, s1, tag=None):
            first = WORD_START[a]
            words = kept([P, s1 - s0], U32, "slot_words%d_%d" % (a, s0), tag)
            gather(words[:], tok_words[:, first : first + window_width(s1 - s0)].bitcast(U32), s0, s1)
            for s in range(s0, s1, C):
                slot_words[a, s // C] = words[:, s - s0 : s - s0 + C].bitcast(FP8X4)

        def last_piece(a):
            return "x_raw%d_%d" % (a, LOAD_CUT[a][-2])

        round_tokens(ORDER[0], 0)
        quantize_tokens(ORDER[0], 0)
        round_tokens(ORDER[0], 1)
        round_tokens(ORDER[0], 2)
        quantize_tokens(ORDER[0], 1)
        quantize_tokens(ORDER[0], 2)
        for a in ORDER[1:]:
            for piece in range(len(x_raw[a])):
                round_tokens(a, piece)

        def gate_col(r, c):
            col = r * CHUNKS + 2 * c % CHUNKS
            return gate_cols[:, col : col + 1]

        turned_gate = bank(P, "turned_gate", 3)
        nc.tensor.transpose(turned_gate[:], gate_rows[:], identity[:])
        nc.scalar.copy(gate_cols[:], turned_gate[:, : TOP * CHUNKS])
        head_width = TURNED * P
        gates = kept([P, TOP, T - head_width], F32, "gates", "x_raw%d_0" % ORDER[LAST])
        for r in range(TOP):
            spread = bank(T - head_width, "spread%d" % r, 4 + r)
            for c in range(TURNED, CHUNKS):
                columns = spread[:, (c - TURNED) * P : (c - TURNED + 1) * P]
                nc.tensor.transpose(columns, gate_col(r, c).to_broadcast([P, P]), identity[:])
            nc.scalar.activation(gates[:, r, :], spread[:], COPY)

        w8_src = w8_words.rearrange("e a p n t -> p e a (n t)").bitcast(I32)
        w4_src = w4_words.rearrange("e a p b -> p e a b").bitcast(I32)
        weights = {}

        def load_weights(e0, e1, a0, a1):
            src, width, dtype = (w8_src, 4, FP8X4) if a0 < HALF else (w4_src, 2, FP4X4)
            tile = kept([P, e1 - e0, a1 - a0, N * width], U8, "w%d_%d" % (e0, a0))
            nc.sync.dma_start(tile[:].bitcast(I32), src[:, e0:e1, a0 % HALF : (a1 - 1) % HALF + 1, :])
            for e in range(e0, e1):
                for a in range(a0, a1):
                    weights[e, a] = tile[:, e - e0, a - a0, :].bitcast(dtype)

        load_weights(0, E, ORDER[0], ORDER[0] + 1)
        for r in range(1, 4):
            nc.sync.dma_start(scale_words[r:P:32, :], scale_words[8 * r : P : 32, :])
        for a in ORDER[1:LAST]:
            load_weights(0, E, a, a + 1)
        for e0, e1 in spans(LAST_CUT):
            load_weights(e0, e1, ORDER[LAST], ORDER[LAST] + 1)

        gather_words(ORDER[0], 0, EARLY[0])
        for piece in range(2):
            quantize_tokens(ORDER[1], piece)
        gather_words(ORDER[0], EARLY[0], S, last_piece(ORDER[1]))
        gather_words(ORDER[1], 0, EARLY[1])
        for i in range(HALF, PASSES):
            for piece in range(2):
                quantize_tokens(ORDER[i], piece)
            gather_words(ORDER[i - 1], EARLY[i - 1], S, last_piece(ORDER[i]))
        gather(slot_scales[:], tok_scales[:], 0, S)
        row = PLANE_ROW[MOVED]
        for q in range(0, P, 32):
            nc.sync.dma_start(last_scales[q : q + 4, :].bitcast(I32), slot_scales[row + q : row + q + 4, :].bitcast(I32))
        for tile, pos in zip(token_slot, (pos1, pos2, pos3)):
            nc.sync.dma_start(tile[:], pos)
        gather_words(ORDER[HALF], 0, EARLY[HALF])

        groups = spans(BANK_CUT)
        sums = [bank((e1 - e0) * C, "sums%d" % b, b) for b, (e0, e1) in enumerate(groups)]

        def multiply(b, a):
            e0, e1 = groups[b]
            for e in range(e0, e1):
                slots = slice(e * C, (e + 1) * C)
                m = (a // HALF * E + e) * HALF + a % HALF
                x_plane = last_scales[:, slots] if a == MOVED else slot_scales[PLANE_ROW[a] : P, slots]
                nc.tensor.matmul_mx(
                    out=sums[b][:, (e - e0) * C : (e - e0 + 1) * C],
                    lhsT=weights[e, a],
                    lhsT_scale=w_scales[:, m * N : (m + 1) * N],
                    rhs=slot_words[a, e],
                    rhs_scale=x_plane,
                    start=(a == ORDER[0] and e == e0),
                    stop=(a == ORDER[LAST] and e == e1 - 1),
                )

        for b in range(len(groups)):
            for a in ORDER[:HALF]:
                multiply(b, a)
        for b in range(len(groups)):
            multiply(b, ORDER[HALF])
        for c0, c1 in spans(CLOSE_CUT):
            gather_words(ORDER[LAST], c0 * C, c1 * C)
            for b, (e0, e1) in enumerate(groups):
                if c0 <= e0 < c1:
                    multiply(b, ORDER[LAST])
                    copy = nc.vector.tensor_copy if e1 == E - 1 else nc.scalar.copy
                    copy(y[:, e0 * C : e1 * C], sums[b][:])

        def offsets(r, t0, t1):
            return token_slot[r][:, t0 // LIST_ROWS : t1 // LIST_ROWS]

        plain = [kept([P, head_width], F32, "plain%d" % r) for r in range(TOP)]
        for r in range(TOP):
            nc.scalar.activation(plain[r][:], y[:].indirect(offsets(r, 0, head_width)), COPY)
        terms = [kept([P, T - head_width], F32, "term%d" % r) for r in range(TOP)]
        for r in range(TOP):
            nc.vector.tensor_tensor(terms[r][:], y[:].indirect(offsets(r, head_width, T)), gates[:, r, :], MULT)

        flipped = {}
        for r in range(TOP):
            for c in range(TURNED):
                flipped[r, c] = bank(P, "flipped%d_%d" % (r, c), r * TURNED + c)
                nc.tensor.transpose(flipped[r, c][:], plain[r][:, c * P : (c + 1) * P], identity[:])
        back = [bank(P, "back%d" % c, TOP * TURNED + c) for c in range(TURNED)]
        for c in range(TURNED):
            for r in range(TOP):
                weighed = kept([P, P], F32, "weighed%d_%d" % (r, c))
                nc.scalar.activation(weighed[:], flipped[r, c][:], COPY, scale=gate_col(r, c))
                nc.tensor.matmul(
                    back[c][:], weighed[:], identity[:], start=(r == 0), stop=(r == TOP - 1), is_transpose=True
                )

        def add(name, in0, in1):
            total = kept(list(in0.shape), F32, name)
            nc.vector.tensor_tensor(total[:], in0, in1, ADD)
            return total

        added = [slice(t0 - head_width, t1 - head_width) for t0, t1 in spans(ADD_CUT)]
        partials = [add("partial%d" % g, terms[0][:, cols], terms[1][:, cols]) for g, cols in enumerate(added)]
        for partial, cols, (t0, t1) in zip(partials, added, spans(ADD_CUT)):
            total = add("total%d" % t0, partial[:], terms[2][:, cols])
            nc.sync.dma_start(out[:, t0:t1], total[:])

        for c in range(TURNED):
            head = kept([P, P], F32, "head%d" % c)
            nc.scalar.copy(head[:], back[c][:])
            nc.sync.dma_start(out[:, c * P : (c + 1) * P], head[:])
